import numpy as np
import ml_dtypes


def mxq(x, axis, fmt="e4m3"):
    dtype, down = {"e4m3": (ml_dtypes.float8_e4m3fn, 7), "e5m2": (ml_dtypes.float8_e5m2, 14)}[fmt]
    v = np.moveaxis(np.asarray(x, np.float32).astype(ml_dtypes.bfloat16).astype(np.float64), axis, -1)
    blocks = v.reshape(v.shape[:-1] + (-1, 32))
    amax = np.abs(blocks).max(-1, keepdims=True)
    byte = np.maximum(np.where(amax > 0, np.frexp(amax)[1] - 1 + 127, 0) - down, 1)
    scale = np.exp2(byte - 127.0)
    codes = (blocks / scale).astype(np.float32).astype(dtype).astype(np.float64)
    return np.moveaxis((codes * scale).reshape(v.shape), -1, axis)


WIDE = False


def mx_kscale(k):
    if not WIDE:
        return np.ones(k)
    levels = np.array([10, -10, 5, -5, 0])
    if k % 512:
        return np.exp2(np.random.permutation(np.resize(levels, k // 32))).repeat(32)
    a = np.empty((k // 512, 16))
    for p in range(k // 512):
        a[p, :8] = np.random.permutation(np.resize(levels, 8))
        for g in range(8):
            far = levels[np.abs(levels - a[p, g]) >= 10]
            a[p, g + 8] = far[np.random.randint(len(far))]
    return np.exp2(a.ravel()).repeat(32)


def f64(x):
    return np.asarray(x).astype(np.float64)


def striped(idx):
    return np.tile(idx.reshape(-1, 16).T, (8, 1)).astype(np.uint16)


def unstriped(offs):
    return offs[:16].T.reshape(-1).astype(np.int64)


E2M1 = np.array([0.0, 0.5, 1.0, 1.5, 2.0, 3.0, 4.0, 6.0, -0.0, -0.5, -1.0, -1.5, -2.0, -3.0, -4.0, -6.0])


def pack_weight(w, fmt):
    k, n = w.shape
    w = f64(np.asarray(w, np.float32).astype(ml_dtypes.bfloat16)).reshape(k // 32, 32, n)
    amax = np.abs(w).max(1)
    if fmt == "e4m3":
        byte = np.frexp(amax)[1] - 1 + 127 - 7
    else:
        mant, ex = np.frexp(amax / 6.0)
        byte = np.where(mant > 0.5, ex, ex - 1) + 127
    byte = np.clip(np.where(amax > 0, byte, 1), 1, 254)
    scaled = (w * np.exp2(127.0 - byte)[:, None, :]).reshape(k, n).astype(np.float32)
    by_word = np.ascontiguousarray(scaled.reshape(k // 512, 128, 4, n).transpose(0, 1, 3, 2))
    if fmt == "e4m3":
        words = by_word.astype(ml_dtypes.float8_e4m3fn).view(np.uint8)
    else:
        c = by_word.astype(ml_dtypes.float4_e2m1fn).view(np.uint8) & 0xF
        words = (c[..., 0::2] | (c[..., 1::2] << 4)).reshape(k // 512, 128, 2 * n)
    return np.ascontiguousarray(words), np.ascontiguousarray(byte.astype(np.uint8).reshape(k // 512, 16, n))


def unpack_weight(words, scales, fmt):
    g, _, n = scales.shape
    words = np.ascontiguousarray(words).reshape(g, 128, n, -1)
    if fmt == "e4m3":
        vals = words.view(ml_dtypes.float8_e4m3fn).astype(np.float64)
    else:
        nib = np.empty((g, 128, n, 4), np.uint8)
        nib[..., 0::2] = words & 0xF
        nib[..., 1::2] = words >> 4
        vals = E2M1[nib]
    vals = vals * np.repeat(np.exp2(scales.astype(np.float64) - 127.0), 8, axis=1)[..., None]
    return vals.transpose(0, 1, 3, 2).reshape(g * 512, n)


def relu(v):
    return np.maximum(v, 0.0)


K, T, E, C, H, N = 512, 512, 12, 128, 512, 128
TOP = 3


def by_expert(wq, xq):
    return np.concatenate([wq[e].T @ xq[:, e * C:(e + 1) * C] for e in range(E)], axis=1)


def setup_inputs():
    n = np.random.standard_normal
    s = mx_kscale(K)[:, None]
    u = mx_kscale(H)
    deal = np.repeat(np.arange(E), C).reshape(TOP, T)[:, np.random.permutation(T)]
    deal = np.take_along_axis(deal, np.argsort(np.random.rand(TOP, T), axis=0), axis=0)
    for _ in range(8):
        s_, t_ = np.random.permutation(T).reshape(2, -1); r = np.random.randint(TOP, size=T // 2); x, y = deal[r, s_].copy(), deal[r, t_].copy()
        ok = ~((deal[:, s_] == y).any(0) | (deal[:, t_] == x).any(0)); deal[r[ok], s_[ok]] = y[ok]; deal[r[ok], t_[ok]] = x[ok]
    order = np.lexsort((np.random.rand(TOP * T), deal.reshape(-1)))
    slot_token = order % T; pos = np.empty(TOP * T, np.int64); pos[order] = np.arange(TOP * T); pos = pos.reshape(TOP, T)
    g = np.random.uniform(0.5, 1.5, (TOP, T)); g = g / g.sum(0)
    w1 = [pack_weight(m, "e2m1") for m in n((E, K, H)) / np.sqrt(K) / s[None]]
    w3 = [pack_weight(m, "e2m1") for m in n((E, K, H)) / np.sqrt(K) / s[None] * u[None, None, :]]
    w2 = [pack_weight(m, "e2m1") for m in n((E, H, N)) / np.sqrt(H) / u[None, :, None]]
    return {
        "xT": (n((K, T)) * s).astype(np.float32),
        "w1_words": np.stack([m[0] for m in w1]),
        "w1_scales": np.stack([m[1] for m in w1]),
        "w3_words": np.stack([m[0] for m in w3]),
        "w3_scales": np.stack([m[1] for m in w3]),
        "w2_words": np.stack([m[0] for m in w2]),
        "w2_scales": np.stack([m[1] for m in w2]),
        "gate": np.stack([np.tile(r, (N, 1)) for r in g]).astype(np.float32),
        "offs": striped(slot_token),
        "pos1": striped(pos[0]),
        "pos2": striped(pos[1]),
        "pos3": striped(pos[2]),
    }


def reference(xT, w1_words, w1_scales, w3_words, w3_scales, w2_words, w2_scales, gate, offs, pos1, pos2, pos3):
    idx = unstriped(offs)
    w1 = np.stack([unpack_weight(w1_words[e], w1_scales[e], "e2m1") for e in range(E)])
    w3 = np.stack([unpack_weight(w3_words[e], w3_scales[e], "e2m1") for e in range(E)])
    w2 = np.stack([unpack_weight(w2_words[e], w2_scales[e], "e2m1") for e in range(E)])
    xq = mxq(f64(xT)[:, idx], 0, "e4m3")
    h = relu(by_expert(w1, xq))
    h = h * by_expert(w3, xq)
    y = by_expert(w2, mxq(h, 0, "e4m3"))
    return sum(f64(gate[r]) * y[:, unstriped(p)] for r, p in enumerate((pos1, pos2, pos3)))

@@ -1,0 +1,218 @@
+from contextlib import ExitStack
+
+import concourse.mybir as mybir
+from concourse.masks import make_identity
+
+K, T, E, C, H, N = 512, 512, 12, 128, 512, 128
+TOP = 3
+S = E * C
+P = 128
+PACK = 4
+
+FLOPS = 2 * S * (2 * K * H + H * N)
+
+F32 = mybir.dt.float32
+BF16 = mybir.dt.bfloat16
+I32 = mybir.dt.int32
+U32 = mybir.dt.uint32
+U16 = mybir.dt.uint16
+U8 = mybir.dt.uint8
+FP8X4 = mybir.dt.float8_e4m3fn_x4
+FP4X4 = mybir.dt.float4_e2m1fn_x4
+MULT = mybir.AluOpType.mult
+ADD = mybir.AluOpType.add
+RELU = mybir.ActivationFunctionType.Relu
+
+GROUPS = [(0,), (1, 2), (3, 4), (5, 6), (7, 8), (9, 10), (11,)]
+PIECES = [(0, 1), (1, 3), (3, 6), (6, 9), (9, 12)]
+EARLY = 3
+X_CHUNKS = [(0, 256, ("scalar", "vector")), (256, 128, ("scalar",)), (384, 128, ("vector",))]
+X_TILE = 256
+CUT = 384
+
+
+def tile_moe_tk_glu_relu_kernel(
+    tc, xT, w1_words, w1_scales, w3_words, w3_scales, w2_words, w2_scales, gate, offs, pos1, pos2, pos3, out
+):
+    nc = tc.nc
+    with ExitStack() as ctx:
+        held = ctx.enter_context(tc.tile_pool(name="held", bufs=1))
+        gathered = ctx.enter_context(tc.tile_pool(name="gathered", bufs=3))
+        products = ctx.enter_context(tc.tile_pool(name="products", bufs=6))
+        hidden = ctx.enter_context(tc.tile_pool(name="hidden", bufs=4))
+        psum = ctx.enter_context(tc.psum_pool(name="psum", bufs=2))
+
+        s1 = held.tile([P, E, H], U8, name="s1", align_bytes=64)
+        s3 = held.tile([P, E, H], U8, name="s3", align_bytes=64)
+        s2 = held.tile([P, E, N], U8, name="s2", align_bytes=64)
+        x_words = held.tile([P, T], U32, name="x_words", align_bytes=64)
+        x_scales = held.tile([P, T], U8, name="x_scales", align_bytes=64)
+        ident = held.tile([P, P], F32, name="ident")
+
+        def zero(engine, scales, e0, e1):
+            engine.memset(scales[:, e0:e1, :].rearrange("p e i -> p (e i)").bitcast(I32), 0)
+
+        zero(nc.vector, s1, 0, EARLY)
+        zero(nc.vector, s3, 0, EARLY)
+        zero(nc.vector, s2, 0, E)
+        nc.gpsimd.memset(x_scales[:], 0)
+        zero(nc.gpsimd, s1, EARLY, E)
+        zero(nc.gpsimd, s3, EARLY, E)
+        make_identity(nc, ident[:])
+
+        x_rows = xT.rearrange("(p j) t -> p j t", j=PACK)
+        x_f32 = []
+        for i, (t0, n, engines) in enumerate(X_CHUNKS):
+            chunk = held.tile([P, PACK, n], F32, name=f"x_f32_{i}")
+            nc.sync.dma_start(chunk[:], x_rows[:, :, t0 : t0 + n])
+            x_f32.append(chunk)
+        offs_sb = held.tile([P, S // 16], U16, name="offs_sb")
+        nc.sync.dma_start(offs_sb[:], offs)
+
+        def load_scales(tile, scales, e0, e1):
+            for q in range(4):
+                nc.sync.dma_start(
+                    tile[32 * q : 32 * q + 4, e0:e1, :].bitcast(I32),
+                    scales[e0:e1, 0, 4 * q : 4 * q + 4, :].rearrange("e q i -> q e i").bitcast(I32),
+                )
+
+        w1_sb, w3_sb = {}, {}
+
+        def load_words(g):
+            for name, words, by_expert in ((f"w1_{g}", w1_words, w1_sb), (f"w3_{g}", w3_words, w3_sb)):
+                e0, n = GROUPS[g][0], len(GROUPS[g])
+                w = held.tile([P, n, 2 * H], U8, name=name, align_bytes=64)
+                nc.sync.dma_start(w[:].bitcast(I32), words[e0 : e0 + n, 0].rearrange("e p b -> p e b").bitcast(I32))
+                for k in range(n):
+                    by_expert[e0 + k] = w[:, k, :]
+
+        load_words(0)
+        load_scales(s1, w1_scales, 0, EARLY)
+        load_scales(s3, w3_scales, 0, EARLY)
+        load_words(1)
+        load_scales(s2, w2_scales, 0, E)
+        w2_sb = held.tile([P, E, 2 * N], U8, name="w2_sb", align_bytes=64)
+        nc.sync.dma_start(w2_sb[:].bitcast(I32), w2_words[:, 0].rearrange("e p b -> p e b").bitcast(I32))
+        load_scales(s1, w1_scales, EARLY, E)
+        load_scales(s3, w3_scales, EARLY, E)
+        for g in range(2, len(GROUPS)):
+            load_words(g)
+        pos_sb = []
+        for r, pos in enumerate((pos1, pos2, pos3)):
+            places = held.tile([P, T // 16], U16, name=f"pos_sb_{r}")
+            nc.sync.dma_start(places[:], pos)
+            pos_sb.append(places)
+        gate_sb = held.tile([P, TOP, T], F32, name="gate_sb")
+        nc.sync.dma_start(gate_sb[:], gate.rearrange("r n t -> n r t"))
+
+        x_bf16 = [held.tile([P, X_TILE, PACK], BF16, name=f"x_bf16_{i}", align_bytes=64) for i in range(T // X_TILE)]
+        for (t0, n, engines), chunk in zip(X_CHUNKS, x_f32):
+            for k, engine in enumerate(engines):
+                rounded = x_bf16[t0 // X_TILE][:, t0 % X_TILE + 128 * k : t0 % X_TILE + 128 * (k + 1), :]
+                rows = chunk[:, :, 128 * k : 128 * (k + 1)].rearrange("p j t -> p t j")
+                if engine == "scalar":
+                    nc.scalar.copy(rounded, rows)
+                else:
+                    nc.vector.tensor_copy(rounded, rows)
+        for i, rounded in enumerate(x_bf16):
+            cols = slice(X_TILE * i, X_TILE * (i + 1))
+            nc.vector.quantize_mx(
+                out=x_words[:, cols].bitcast(FP8X4),
+                scales=x_scales[:, cols],
+                in_=rounded[:].rearrange("p t j -> p (t j)"),
+            )
+
+        codes_of, scales_of = {}, {}
+
+        def gather(e0, e1):
+            n = e1 - e0
+            listed = offs_sb[:, e0 * C // 16 : e1 * C // 16]
+            codes = gathered.tile([P, n * C], U32, name="codes", align_bytes=64)
+            scales = gathered.tile([P, n * C], U8, name="scales", align_bytes=64)
+            nc.vector.tensor_copy(codes[:], x_words[:].indirect(listed))
+            nc.vector.tensor_copy(scales[:], x_scales[:].indirect(listed))
+            for k in range(n):
+                codes_of[e0 + k] = codes[:, k * C : (k + 1) * C]
+                scales_of[e0 + k] = scales[:, k * C : (k + 1) * C]
+
+        def by_pairs(acc):
+            return acc.rearrange("c (p u v) -> c u p v", u=2, v=2)
+
+        h_of = {}
+
+        def first_layer(g):
+            for e in GROUPS[g]:
+                a = psum.tile([C, H], F32, name="a")
+                b = psum.tile([C, H], F32, name="b")
+                for acc, w, s in ((a, w1_sb, s1), (b, w3_sb, s3)):
+                    nc.tensor.matmul_mx(
+                        out=acc[:],
+                        lhsT=codes_of[e].bitcast(FP8X4),
+                        lhsT_scale=scales_of[e],
+                        rhs=w[e].bitcast(FP4X4),
+                        rhs_scale=s[:, e, :],
+                        start=True,
+                        stop=True,
+                    )
+                relu_a = products.tile([C, 2, P, 2], F32, name="relu_a")
+                nc.scalar.activation(relu_a[:], by_pairs(a[:]), RELU)
+                h = products.tile([C, 2, P, 2], BF16, name="h")
+                nc.vector.tensor_tensor(h[:], by_pairs(b[:]), relu_a[:], MULT)
+                h_of[e] = h
+
+        y_all = held.tile([N, S], F32, name="y_all")
+
+        def second_layer(g):
+            e0, n = GROUPS[g][0], len(GROUPS[g])
+            empty = nc.vector.tensor_copy if g == len(GROUPS) - 1 else nc.scalar.copy
+
+            turned = psum.tile([P, n, 2, C], F32, name="turned")
+            for k, e in enumerate(GROUPS[g]):
+                words = h_of[e][:].rearrange("c u p v -> c (u p v)").bitcast(F32)
+                for u in range(2):
+                    nc.tensor.transpose(turned[:, k, u, :], words[:, u * P : (u + 1) * P], ident[:])
+            h_rows = hidden.tile([P, n, C, PACK], BF16, name="h_rows", align_bytes=64)
+            empty(h_rows[:].bitcast(F32), turned[:].rearrange("p k u c -> p k c u"))
+
+            h_codes = hidden.tile([P, n * C], U32, name="h_codes", align_bytes=64)
+            h_scales = hidden.tile([P, n * C], U8, name="h_scales", align_bytes=64)
+            nc.vector.quantize_mx(
+                out=h_codes[:].bitcast(FP8X4),
+                scales=h_scales[:],
+                in_=h_rows[:].rearrange("p k c j -> p (k c j)"),
+            )
+            y = psum.tile([N, n * C], F32, name="y")
+            for k, e in enumerate(GROUPS[g]):
+                mine = slice(k * C, (k + 1) * C)
+                nc.tensor.matmul_mx(
+                    out=y[:, mine],
+                    lhsT=w2_sb[:, e, :].bitcast(FP4X4),
+                    lhsT_scale=s2[:, e, :],
+                    rhs=h_codes[:, mine].bitcast(FP8X4),
+                    rhs_scale=h_scales[:, mine],
+                    start=True,
+                    stop=True,
+                )
+            empty(y_all[:, e0 * C : (e0 + n) * C], y[:])
+
+        fetched = 0
+        for g in range(len(GROUPS)):
+            ahead = GROUPS[min(g + 1, len(GROUPS) - 1)][-1]
+            for e0, e1 in PIECES:
+                if fetched == e0 and e0 <= ahead:
+                    gather(e0, e1)
+                    fetched = e1
+            first_layer(g)
+            if g > 0:
+                second_layer(g - 1)
+        second_layer(len(GROUPS) - 1)
+
+        parts = [held.tile([N, T], F32, name=f"part_{r}") for r in range(TOP)]
+        for r in range(TOP):
+            nc.vector.tensor_tensor(parts[r][:], y_all[:].indirect(pos_sb[r][:]), gate_sb[:, r, :], MULT)
+        two = held.tile([N, T], F32, name="two")
+        total = held.tile([N, T], F32, name="total")
+        nc.vector.tensor_tensor(two[:], parts[0][:], parts[1][:], ADD)
+        for t0, t1 in ((0, CUT), (CUT, T)):
+            nc.vector.tensor_tensor(total[:, t0:t1], two[:, t0:t1], parts[2][:, t0:t1], ADD)
+            nc.sync.dma_start(out[:, t0:t1], total[:, t0:t1])

@@ -25,7 +25,8 @@ RELU = mybir.ActivationFunctionType.Relu
 
 GROUPS = [(0,), (1, 2), (3, 4), (5, 6), (7, 8), (9, 10), (11,)]
 PIECES = [(0, 1), (1, 3), (3, 6), (6, 9), (9, 12)]
-EARLY = 3
+RANGES = [(0, 5), (5, E)]
+A_BANKS, B_BANKS, TURNED_BANKS, Y_BANKS = 2, 2, 2, 2
 X_CHUNKS = [(0, 256, ("scalar", "vector")), (256, 128, ("scalar",)), (384, 128, ("vector",))]
 X_TILE = 256
 CUT = 384
@@ -40,24 +41,25 @@ def tile_moe_tk_glu_relu_kernel(
         gathered = ctx.enter_context(tc.tile_pool(name="gathered", bufs=3))
         products = ctx.enter_context(tc.tile_pool(name="products", bufs=6))
         hidden = ctx.enter_context(tc.tile_pool(name="hidden", bufs=4))
-        psum = ctx.enter_context(tc.psum_pool(name="psum", bufs=2))
+        psum = ctx.enter_context(tc.psum_pool(name="psum", bufs=1))
 
-        s1 = held.tile([P, E, H], U8, name="s1", align_bytes=64)
-        s3 = held.tile([P, E, H], U8, name="s3", align_bytes=64)
+        s1 = [held.tile([P, e1 - e0, H], U8, name=f"s1_{e0}", align_bytes=64) for e0, e1 in RANGES]
+        s3 = [held.tile([P, e1 - e0, H], U8, name=f"s3_{e0}", align_bytes=64) for e0, e1 in RANGES]
         s2 = held.tile([P, E, N], U8, name="s2", align_bytes=64)
         x_words = held.tile([P, T], U32, name="x_words", align_bytes=64)
         x_scales = held.tile([P, T], U8, name="x_scales", align_bytes=64)
         ident = held.tile([P, P], F32, name="ident")
 
-        def zero(engine, scales, e0, e1):
-            engine.memset(scales[:, e0:e1, :].rearrange("p e i -> p (e i)").bitcast(I32), 0)
+        def zero(engine, scales):
+            engine.memset(scales[:].rearrange("p e i -> p (e i)").bitcast(I32), 0)
 
-        zero(nc.vector, s1, 0, EARLY)
-        zero(nc.vector, s3, 0, EARLY)
-        zero(nc.vector, s2, 0, E)
+        zero(nc.gpsimd, s1[0])
+        zero(nc.vector, s3[0])
+        zero(nc.vector, s2)
         nc.gpsimd.memset(x_scales[:], 0)
-        zero(nc.gpsimd, s1, EARLY, E)
-        zero(nc.gpsimd, s3, EARLY, E)
+        for i in range(1, len(RANGES)):
+            zero(nc.vector, s1[i])
+            zero(nc.gpsimd, s3[i])
         make_identity(nc, ident[:])
 
         x_rows = xT.rearrange("(p j) t -> p j t", j=PACK)
@@ -70,11 +72,9 @@ def tile_moe_tk_glu_relu_kernel(
         nc.sync.dma_start(offs_sb[:], offs)
 
         def load_scales(tile, scales, e0, e1):
-            for q in range(4):
-                nc.sync.dma_start(
-                    tile[32 * q : 32 * q + 4, e0:e1, :].bitcast(I32),
-                    scales[e0:e1, 0, 4 * q : 4 * q + 4, :].rearrange("e q i -> q e i").bitcast(I32),
-                )
+            rows = scales[e0:e1, 0].rearrange("e (q r) i -> r q e i", r=4)
+            for r in range(4):
+                nc.sync.dma_start(tile[r:P:32, :, :].bitcast(I32), rows[r].bitcast(I32))
 
         w1_sb, w3_sb = {}, {}
 
@@ -87,15 +87,16 @@ def tile_moe_tk_glu_relu_kernel(
                     by_expert[e0 + k] = w[:, k, :]
 
         load_words(0)
-        load_scales(s1, w1_scales, 0, EARLY)
-        load_scales(s3, w3_scales, 0, EARLY)
+        load_scales(s1[0], w1_scales, *RANGES[0])
+        load_scales(s3[0], w3_scales, *RANGES[0])
         load_words(1)
+        load_words(2)
         load_scales(s2, w2_scales, 0, E)
         w2_sb = held.tile([P, E, 2 * N], U8, name="w2_sb", align_bytes=64)
         nc.sync.dma_start(w2_sb[:].bitcast(I32), w2_words[:, 0].rearrange("e p b -> p e b").bitcast(I32))
-        load_scales(s1, w1_scales, EARLY, E)
-        load_scales(s3, w3_scales, EARLY, E)
-        for g in range(2, len(GROUPS)):
+        load_scales(s1[1], w1_scales, *RANGES[1])
+        load_scales(s3[1], w3_scales, *RANGES[1])
+        for g in range(3, len(GROUPS)):
             load_words(g)
         pos_sb = []
         for r, pos in enumerate((pos1, pos2, pos3)):
@@ -142,15 +143,16 @@ def tile_moe_tk_glu_relu_kernel(
 
         def first_layer(g):
             for e in GROUPS[g]:
-                a = psum.tile([C, H], F32, name="a")
-                b = psum.tile([C, H], F32, name="b")
+                a = psum.tile([C, H], F32, name="a", bufs=A_BANKS)
+                b = psum.tile([C, H], F32, name="b", bufs=B_BANKS)
+                i = [e0 <= e < e1 for e0, e1 in RANGES].index(True)
                 for acc, w, s in ((a, w1_sb, s1), (b, w3_sb, s3)):
                     nc.tensor.matmul_mx(
                         out=acc[:],
                         lhsT=codes_of[e].bitcast(FP8X4),
                         lhsT_scale=scales_of[e],
                         rhs=w[e].bitcast(FP4X4),
-                        rhs_scale=s[:, e, :],
+                        rhs_scale=s[i][:, e - RANGES[i][0], :],
                         start=True,
                         stop=True,
                     )
@@ -166,7 +168,7 @@ def tile_moe_tk_glu_relu_kernel(
             e0, n = GROUPS[g][0], len(GROUPS[g])
             empty = nc.vector.tensor_copy if g == len(GROUPS) - 1 else nc.scalar.copy
 
-            turned = psum.tile([P, n, 2, C], F32, name="turned")
+            turned = psum.tile([P, n, 2, C], F32, name="turned", bufs=TURNED_BANKS)
             for k, e in enumerate(GROUPS[g]):
                 words = h_of[e][:].rearrange("c u p v -> c (u p v)").bitcast(F32)
                 for u in range(2):
@@ -181,7 +183,7 @@ def tile_moe_tk_glu_relu_kernel(
                 scales=h_scales[:],
                 in_=h_rows[:].rearrange("p k c j -> p (k c j)"),
             )
-            y = psum.tile([N, n * C], F32, name="y")
+            y = psum.tile([N, n * C], F32, name="y", bufs=Y_BANKS)
             for k, e in enumerate(GROUPS[g]):
                 mine = slice(k * C, (k + 1) * C)
                 nc.tensor.matmul_mx(

@@ -23,12 +23,18 @@ MULT = mybir.AluOpType.mult
 ADD = mybir.AluOpType.add
 RELU = mybir.ActivationFunctionType.Relu
 
-GROUPS = [(0,), (1, 2), (3, 4), (5, 6), (7, 8), (9, 10), (11,)]
-PIECES = [(0, 1), (1, 3), (3, 6), (6, 9), (9, 12)]
-RANGES = [(0, 5), (5, E)]
+LOADS = [(0, 1), (2, 3, 4), (5, 6, 7), (8, 9), (10, 11)]
+Y_GROUPS = [(0, 1, 2, 3), (4, 5, 6, 7), (8, 9, 10), (11,)]
+TURN_GROUPS = [(0, 1), (2, 3), (4, 5), (6, 7), (8,), (9,), (10,), (11,)]
+AHEAD = 8
+LATE = 11
+RANGES = [(0, E)]
+LAG = 2
+LAG2 = 4
 A_BANKS, B_BANKS, TURNED_BANKS, Y_BANKS = 2, 2, 2, 2
-X_CHUNKS = [(0, 256, ("scalar", "vector")), (256, 128, ("scalar",)), (384, 128, ("vector",))]
 X_TILE = 256
+X_VECTOR = 160
+W2_EARLY = 6
 CUT = 384
 
 
@@ -38,9 +44,9 @@ def tile_moe_tk_glu_relu_kernel(
     nc = tc.nc
     with ExitStack() as ctx:
         held = ctx.enter_context(tc.tile_pool(name="held", bufs=1))
-        gathered = ctx.enter_context(tc.tile_pool(name="gathered", bufs=3))
-        products = ctx.enter_context(tc.tile_pool(name="products", bufs=6))
-        hidden = ctx.enter_context(tc.tile_pool(name="hidden", bufs=4))
+        gathered = ctx.enter_context(tc.tile_pool(name="gathered", bufs=AHEAD))
+        products = ctx.enter_context(tc.tile_pool(name="products", bufs=E))
+        hidden = ctx.enter_context(tc.tile_pool(name="hidden", bufs=len(TURN_GROUPS)))
         psum = ctx.enter_context(tc.psum_pool(name="psum", bufs=1))
 
         s1 = [held.tile([P, e1 - e0, H], U8, name=f"s1_{e0}", align_bytes=64) for e0, e1 in RANGES]
@@ -50,23 +56,22 @@ def tile_moe_tk_glu_relu_kernel(
         x_scales = held.tile([P, T], U8, name="x_scales", align_bytes=64)
         ident = held.tile([P, P], F32, name="ident")
 
-        def zero(engine, scales):
-            engine.memset(scales[:].rearrange("p e i -> p (e i)").bitcast(I32), 0)
+        def words_of(scales):
+            return scales[:].rearrange("p e i -> p (e i)").bitcast(I32)
 
-        zero(nc.gpsimd, s1[0])
-        zero(nc.vector, s3[0])
-        zero(nc.vector, s2)
+        for scales in (s1[0], s3[0]):
+            half = words_of(scales).shape[1] // 2
+            nc.gpsimd.memset(words_of(scales)[:, :half], 0)
+            nc.vector.memset(words_of(scales)[:, half:], 0)
+        nc.vector.memset(words_of(s2), 0)
         nc.gpsimd.memset(x_scales[:], 0)
-        for i in range(1, len(RANGES)):
-            zero(nc.vector, s1[i])
-            zero(nc.gpsimd, s3[i])
         make_identity(nc, ident[:])
 
         x_rows = xT.rearrange("(p j) t -> p j t", j=PACK)
         x_f32 = []
-        for i, (t0, n, engines) in enumerate(X_CHUNKS):
-            chunk = held.tile([P, PACK, n], F32, name=f"x_f32_{i}")
-            nc.sync.dma_start(chunk[:], x_rows[:, :, t0 : t0 + n])
+        for t0 in range(0, T, X_TILE):
+            chunk = held.tile([P, PACK, X_TILE], F32, name=f"x_f32_{t0}")
+            nc.sync.dma_start(chunk[:], x_rows[:, :, t0 : t0 + X_TILE])
             x_f32.append(chunk)
         offs_sb = held.tile([P, S // 16], U16, name="offs_sb")
         nc.sync.dma_start(offs_sb[:], offs)
@@ -76,28 +81,30 @@ def tile_moe_tk_glu_relu_kernel(
             for r in range(4):
                 nc.sync.dma_start(tile[r:P:32, :, :].bitcast(I32), rows[r].bitcast(I32))
 
-        w1_sb, w3_sb = {}, {}
+        w1_sb, w3_sb, w2_sb = {}, {}, {}
 
-        def load_words(g):
-            for name, words, by_expert in ((f"w1_{g}", w1_words, w1_sb), (f"w3_{g}", w3_words, w3_sb)):
-                e0, n = GROUPS[g][0], len(GROUPS[g])
-                w = held.tile([P, n, 2 * H], U8, name=name, align_bytes=64)
-                nc.sync.dma_start(w[:].bitcast(I32), words[e0 : e0 + n, 0].rearrange("e p b -> p e b").bitcast(I32))
-                for k in range(n):
-                    by_expert[e0 + k] = w[:, k, :]
+        def load_words(name, words, by_expert, width, experts):
+            e0, n = experts[0], len(experts)
+            w = held.tile([P, n, 2 * width], U8, name=f"{name}_{e0}", align_bytes=64)
+            nc.sync.dma_start(w[:].bitcast(I32), words[e0 : e0 + n, 0].rearrange("e p b -> p e b").bitcast(I32))
+            for k in range(n):
+                by_expert[e0 + k] = w[:, k, :]
 
-        load_words(0)
+        def load_first_layer(experts):
+            load_words("w1", w1_words, w1_sb, H, experts)
+            load_words("w3", w3_words, w3_sb, H, experts)
+
+        load_words("w1", w1_words, w1_sb, H, LOADS[0])
         load_scales(s1[0], w1_scales, *RANGES[0])
-        load_scales(s3[0], w3_scales, *RANGES[0])
-        load_words(1)
-        load_words(2)
+        load_words("w3", w3_words, w3_sb, H, LOADS[0])
         load_scales(s2, w2_scales, 0, E)
-        w2_sb = held.tile([P, E, 2 * N], U8, name="w2_sb", align_bytes=64)
-        nc.sync.dma_start(w2_sb[:].bitcast(I32), w2_words[:, 0].rearrange("e p b -> p e b").bitcast(I32))
-        load_scales(s1[1], w1_scales, *RANGES[1])
-        load_scales(s3[1], w3_scales, *RANGES[1])
-        for g in range(3, len(GROUPS)):
-            load_words(g)
+        load_scales(s3[0], w3_scales, *RANGES[0])
+        load_first_layer(LOADS[1])
+        load_first_layer(LOADS[2])
+        load_words("w2", w2_words, w2_sb, N, range(W2_EARLY))
+        load_first_layer(LOADS[3])
+        load_words("w2", w2_words, w2_sb, N, range(W2_EARLY, E))
+        load_first_layer(LOADS[4])
         pos_sb = []
         for r, pos in enumerate((pos1, pos2, pos3)):
             places = held.tile([P, T // 16], U16, name=f"pos_sb_{r}")
@@ -107,14 +114,10 @@ def tile_moe_tk_glu_relu_kernel(
         nc.sync.dma_start(gate_sb[:], gate.rearrange("r n t -> n r t"))
 
         x_bf16 = [held.tile([P, X_TILE, PACK], BF16, name=f"x_bf16_{i}", align_bytes=64) for i in range(T // X_TILE)]
-        for (t0, n, engines), chunk in zip(X_CHUNKS, x_f32):
-            for k, engine in enumerate(engines):
-                rounded = x_bf16[t0 // X_TILE][:, t0 % X_TILE + 128 * k : t0 % X_TILE + 128 * (k + 1), :]
-                rows = chunk[:, :, 128 * k : 128 * (k + 1)].rearrange("p j t -> p t j")
-                if engine == "scalar":
-                    nc.scalar.copy(rounded, rows)
-                else:
-                    nc.vector.tensor_copy(rounded, rows)
+        for rounded, chunk in zip(x_bf16, x_f32):
+            rows = chunk[:].rearrange("p j t -> p t j")
+            nc.vector.tensor_copy(rounded[:, :X_VECTOR, :], rows[:, :X_VECTOR, :])
+            nc.scalar.copy(rounded[:, X_VECTOR:, :], rows[:, X_VECTOR:, :])
         for i, rounded in enumerate(x_bf16):
             cols = slice(X_TILE * i, X_TILE * (i + 1))
             nc.vector.quantize_mx(
@@ -125,55 +128,52 @@ def tile_moe_tk_glu_relu_kernel(
 
         codes_of, scales_of = {}, {}
 
-        def gather(e0, e1):
-            n = e1 - e0
-            listed = offs_sb[:, e0 * C // 16 : e1 * C // 16]
-            codes = gathered.tile([P, n * C], U32, name="codes", align_bytes=64)
-            scales = gathered.tile([P, n * C], U8, name="scales", align_bytes=64)
-            nc.vector.tensor_copy(codes[:], x_words[:].indirect(listed))
-            nc.vector.tensor_copy(scales[:], x_scales[:].indirect(listed))
-            for k in range(n):
-                codes_of[e0 + k] = codes[:, k * C : (k + 1) * C]
-                scales_of[e0 + k] = scales[:, k * C : (k + 1) * C]
+        def gather(e):
+            listed = offs_sb[:, e * C // 16 : (e + 1) * C // 16]
+            codes_of[e] = gathered.tile([P, C], U32, name="codes", align_bytes=64)
+            scales_of[e] = gathered.tile([P, C], U8, name="scales", align_bytes=64)
+            nc.vector.tensor_copy(codes_of[e][:], x_words[:].indirect(listed))
+            nc.vector.tensor_copy(scales_of[e][:], x_scales[:].indirect(listed))
 
         def by_pairs(acc):
             return acc.rearrange("c (p u v) -> c u p v", u=2, v=2)
 
         h_of = {}
 
-        def first_layer(g):
-            for e in GROUPS[g]:
-                a = psum.tile([C, H], F32, name="a", bufs=A_BANKS)
-                b = psum.tile([C, H], F32, name="b", bufs=B_BANKS)
-                i = [e0 <= e < e1 for e0, e1 in RANGES].index(True)
-                for acc, w, s in ((a, w1_sb, s1), (b, w3_sb, s3)):
-                    nc.tensor.matmul_mx(
-                        out=acc[:],
-                        lhsT=codes_of[e].bitcast(FP8X4),
-                        lhsT_scale=scales_of[e],
-                        rhs=w[e].bitcast(FP4X4),
-                        rhs_scale=s[i][:, e - RANGES[i][0], :],
-                        start=True,
-                        stop=True,
-                    )
-                relu_a = products.tile([C, 2, P, 2], F32, name="relu_a")
-                nc.scalar.activation(relu_a[:], by_pairs(a[:]), RELU)
-                h = products.tile([C, 2, P, 2], BF16, name="h")
-                nc.vector.tensor_tensor(h[:], by_pairs(b[:]), relu_a[:], MULT)
-                h_of[e] = h
+        def first_layer(e):
+            a = psum.tile([C, H], F32, name="a", bufs=A_BANKS)
+            b = psum.tile([C, H], F32, name="b", bufs=B_BANKS)
+            i = [e0 <= e < e1 for e0, e1 in RANGES].index(True)
+            for acc, w, s in ((a, w1_sb, s1), (b, w3_sb, s3)):
+                nc.tensor.matmul_mx(
+                    out=acc[:],
+                    lhsT=codes_of[e][:].bitcast(FP8X4),
+                    lhsT_scale=scales_of[e][:],
+                    rhs=w[e].bitcast(FP4X4),
+                    rhs_scale=s[i][:, e - RANGES[i][0], :],
+                    start=True,
+                    stop=True,
+                )
+            relu_a = products.tile([C, 2, P, 2], F32, name="relu_a")
+            nc.scalar.activation(relu_a[:], by_pairs(a[:]), RELU)
+            h = products.tile([C, 2, P, 2], BF16, name="h")
+            nc.vector.tensor_tensor(h[:], by_pairs(b[:]), relu_a[:], MULT)
+            h_of[e] = h
 
         y_all = held.tile([N, S], F32, name="y_all")
+        y_of = {}
 
-        def second_layer(g):
-            e0, n = GROUPS[g][0], len(GROUPS[g])
-            empty = nc.vector.tensor_copy if g == len(GROUPS) - 1 else nc.scalar.copy
+        h_mx = {}
 
+        def turn_and_quantise(group):
+            n = len(group)
             turned = psum.tile([P, n, 2, C], F32, name="turned", bufs=TURNED_BANKS)
-            for k, e in enumerate(GROUPS[g]):
+            for k, e in enumerate(group):
                 words = h_of[e][:].rearrange("c u p v -> c (u p v)").bitcast(F32)
                 for u in range(2):
                     nc.tensor.transpose(turned[:, k, u, :], words[:, u * P : (u + 1) * P], ident[:])
             h_rows = hidden.tile([P, n, C, PACK], BF16, name="h_rows", align_bytes=64)
+            empty = nc.vector.tensor_copy if group[0] >= LATE else nc.scalar.copy
             empty(h_rows[:].bitcast(F32), turned[:].rearrange("p k u c -> p k c u"))
 
             h_codes = hidden.tile([P, n * C], U32, name="h_codes", align_bytes=64)
@@ -183,31 +183,42 @@ def tile_moe_tk_glu_relu_kernel(
                 scales=h_scales[:],
                 in_=h_rows[:].rearrange("p k c j -> p (k c j)"),
             )
-            y = psum.tile([N, n * C], F32, name="y", bufs=Y_BANKS)
-            for k, e in enumerate(GROUPS[g]):
-                mine = slice(k * C, (k + 1) * C)
-                nc.tensor.matmul_mx(
-                    out=y[:, mine],
-                    lhsT=w2_sb[:, e, :].bitcast(FP4X4),
-                    lhsT_scale=s2[:, e, :],
-                    rhs=h_codes[:, mine].bitcast(FP8X4),
-                    rhs_scale=h_scales[:, mine],
-                    start=True,
-                    stop=True,
-                )
-            empty(y_all[:, e0 * C : (e0 + n) * C], y[:])
+            for k, e in enumerate(group):
+                h_mx[e] = (h_codes[:, k * C : (k + 1) * C], h_scales[:, k * C : (k + 1) * C])
 
-        fetched = 0
-        for g in range(len(GROUPS)):
-            ahead = GROUPS[min(g + 1, len(GROUPS) - 1)][-1]
-            for e0, e1 in PIECES:
-                if fetched == e0 and e0 <= ahead:
-                    gather(e0, e1)
-                    fetched = e1
-            first_layer(g)
-            if g > 0:
-                second_layer(g - 1)
-        second_layer(len(GROUPS) - 1)
+        def second_layer(e):
+            h_codes, h_scales = h_mx[e]
+            group = [g for g in Y_GROUPS if e in g][0]
+            if e == group[0]:
+                y_of[e] = psum.tile([N, len(group) * C], F32, name="y", bufs=Y_BANKS)
+            y = y_of[group[0]]
+            nc.tensor.matmul_mx(
+                out=y[:, (e - group[0]) * C : (e - group[0] + 1) * C],
+                lhsT=w2_sb[e].bitcast(FP4X4),
+                lhsT_scale=s2[:, e, :],
+                rhs=h_codes.bitcast(FP8X4),
+                rhs_scale=h_scales,
+                start=True,
+                stop=True,
+            )
+            if e == group[-1]:
+                empty = nc.vector.tensor_copy if e == E - 1 else nc.scalar.copy
+                empty(y_all[:, group[0] * C : (e + 1) * C], y[:])
+
+        for e in range(AHEAD):
+            gather(e)
+        for e in range(E + LAG2):
+            if e < E:
+                first_layer(e)
+            for group in TURN_GROUPS:
+                if group[-1] + LAG == e:
+                    turn_and_quantise(group)
+            for group in TURN_GROUPS:
+                if group[-1] + LAG2 == e:
+                    for done in group:
+                        second_layer(done)
+            if e + AHEAD < E:
+                gather(e + AHEAD)
 
         parts = [held.tile([N, T], F32, name=f"part_{r}") for r in range(TOP)]
         for r in range(TOP):

@@ -23,12 +23,12 @@ MULT = mybir.AluOpType.mult
 ADD = mybir.AluOpType.add
 RELU = mybir.ActivationFunctionType.Relu
 
-LOADS = [(0, 1), (2, 3, 4), (5, 6, 7), (8, 9), (10, 11)]
+LOADS = [(0, 1), (2, 3, 4), (5, 6, 7), (8, 9, 10, 11)]
 Y_GROUPS = [(0, 1, 2, 3), (4, 5, 6, 7), (8, 9, 10), (11,)]
-TURN_GROUPS = [(0, 1), (2, 3), (4, 5), (6, 7), (8,), (9,), (10,), (11,)]
-AHEAD = 8
+TURN_GROUPS = [(e,) for e in range(E)]
+AHEAD = 5
 LATE = 11
-RANGES = [(0, E)]
+RANGES = [(0, 5), (5, E)]
 LAG = 2
 LAG2 = 4
 A_BANKS, B_BANKS, TURNED_BANKS, Y_BANKS = 2, 2, 2, 2
@@ -65,6 +65,8 @@ def tile_moe_tk_glu_relu_kernel(
             nc.vector.memset(words_of(scales)[:, half:], 0)
         nc.vector.memset(words_of(s2), 0)
         nc.gpsimd.memset(x_scales[:], 0)
+        nc.vector.memset(words_of(s1[1]), 0)
+        nc.vector.memset(words_of(s3[1]), 0)
         make_identity(nc, ident[:])
 
         x_rows = xT.rearrange("(p j) t -> p j t", j=PACK)
@@ -97,14 +99,14 @@ def tile_moe_tk_glu_relu_kernel(
         load_words("w1", w1_words, w1_sb, H, LOADS[0])
         load_scales(s1[0], w1_scales, *RANGES[0])
         load_words("w3", w3_words, w3_sb, H, LOADS[0])
-        load_scales(s2, w2_scales, 0, E)
         load_scales(s3[0], w3_scales, *RANGES[0])
         load_first_layer(LOADS[1])
+        load_scales(s1[1], w1_scales, *RANGES[1])
+        load_scales(s3[1], w3_scales, *RANGES[1])
         load_first_layer(LOADS[2])
-        load_words("w2", w2_words, w2_sb, N, range(W2_EARLY))
         load_first_layer(LOADS[3])
-        load_words("w2", w2_words, w2_sb, N, range(W2_EARLY, E))
-        load_first_layer(LOADS[4])
+        load_scales(s2, w2_scales, 0, E)
+        load_words("w2", w2_words, w2_sb, N, range(E))
         pos_sb = []
         for r, pos in enumerate((pos1, pos2, pos3)):
             places = held.tile([P, T // 16], U16, name=f"pos_sb_{r}")
@@ -190,7 +192,10 @@ def tile_moe_tk_glu_relu_kernel(
             h_codes, h_scales = h_mx[e]
             group = [g for g in Y_GROUPS if e in g][0]
             if e == group[0]:
-                y_of[e] = psum.tile([N, len(group) * C], F32, name="y", bufs=Y_BANKS)
+                if Y_GROUPS.index(group) < Y_BANKS:
+                    y_of[e] = psum.tile([N, len(group) * C], F32, name="y", bufs=Y_BANKS)
+                else:
+                    y_of[e] = psum.tile([N, len(group) * C], F32, name="y_late", tag="a", bufs=A_BANKS)
             y = y_of[group[0]]
             nc.tensor.matmul_mx(
                 out=y[:, (e - group[0]) * C : (e - group[0] + 1) * C],
@@ -202,7 +207,7 @@ def tile_moe_tk_glu_relu_kernel(
                 stop=True,
             )
             if e == group[-1]:
-                empty = nc.vector.tensor_copy if e == E - 1 else nc.scalar.copy
+                empty = nc.vector.tensor_copy if Y_GROUPS.index(group) % 2 else nc.scalar.copy
                 empty(y_all[:, group[0] * C : (e + 1) * C], y[:])
 
         for e in range(AHEAD):
@@ -221,11 +226,18 @@ def tile_moe_tk_glu_relu_kernel(
                 gather(e + AHEAD)
 
         parts = [held.tile([N, T], F32, name=f"part_{r}") for r in range(TOP)]
-        for r in range(TOP):
-            nc.vector.tensor_tensor(parts[r][:], y_all[:].indirect(pos_sb[r][:]), gate_sb[:, r, :], MULT)
         two = held.tile([N, T], F32, name="two")
         total = held.tile([N, T], F32, name="total")
+
+        def fetch(r, t0, t1):
+            listed = pos_sb[r][:, t0 // 16 : t1 // 16]
+            nc.vector.tensor_tensor(parts[r][:, t0:t1], y_all[:].indirect(listed), gate_sb[:, r, t0:t1], MULT)
+
+        fetch(0, 0, T)
+        fetch(1, 0, T)
+        fetch(2, 0, CUT)
         nc.vector.tensor_tensor(two[:], parts[0][:], parts[1][:], ADD)
+        fetch(2, CUT, T)
         for t0, t1 in ((0, CUT), (CUT, T)):
             nc.vector.tensor_tensor(total[:, t0:t1], two[:, t0:t1], parts[2][:, t0:t1], ADD)
             nc.sync.dma_start(out[:, t0:t1], total[:, t0:t1])

@@ -23,15 +23,16 @@ MULT = mybir.AluOpType.mult
 ADD = mybir.AluOpType.add
 RELU = mybir.ActivationFunctionType.Relu
 
-LOADS = [(0, 1), (2, 3, 4), (5, 6, 7), (8, 9, 10, 11)]
-Y_GROUPS = [(0, 1, 2, 3), (4, 5, 6, 7), (8, 9, 10), (11,)]
-TURN_GROUPS = [(e,) for e in range(E)]
+LOADS = [(0,), (1, 2), (3, 4, 5), (6, 7), (8, 9), (10, 11)]
+Y_GROUPS = [(0, 1, 2, 3), (4, 5, 6), (7, 8), (9, 10), (11,)]
+TURN_GROUPS = [(0,), (1, 2), (3, 4), (5, 6), (7, 8), (9, 10), (11,)]
 AHEAD = 5
 LATE = 11
-RANGES = [(0, 5), (5, E)]
-LAG = 2
-LAG2 = 4
-A_BANKS, B_BANKS, TURNED_BANKS, Y_BANKS = 2, 2, 2, 2
+RANGES = [(0, 6), (6, E)]
+LAG = 3
+LAG2 = 5
+A_BANKS, B_BANKS, TURNED_BANKS, Y_BANKS = 2, 3, 2, 1
+Y_PLACES = [("y", Y_BANKS), ("b", B_BANKS), ("a", A_BANKS), ("a", A_BANKS), ("b", B_BANKS)]
 X_TILE = 256
 X_VECTOR = 160
 W2_EARLY = 6
@@ -101,10 +102,13 @@ def tile_moe_tk_glu_relu_kernel(
         load_words("w3", w3_words, w3_sb, H, LOADS[0])
         load_scales(s3[0], w3_scales, *RANGES[0])
         load_first_layer(LOADS[1])
-        load_scales(s1[1], w1_scales, *RANGES[1])
-        load_scales(s3[1], w3_scales, *RANGES[1])
         load_first_layer(LOADS[2])
-        load_first_layer(LOADS[3])
+        load_scales(s1[1], w1_scales, *RANGES[1])
+        load_words("w1", w1_words, w1_sb, H, LOADS[3])
+        load_scales(s3[1], w3_scales, *RANGES[1])
+        load_words("w3", w3_words, w3_sb, H, LOADS[3])
+        for experts in LOADS[4:]:
+            load_first_layer(experts)
         load_scales(s2, w2_scales, 0, E)
         load_words("w2", w2_words, w2_sb, N, range(E))
         pos_sb = []
@@ -170,7 +174,7 @@ def tile_moe_tk_glu_relu_kernel(
         def turn_and_quantise(group):
             n = len(group)
             turned = psum.tile([P, n, 2, C], F32, name="turned", bufs=TURNED_BANKS)
-            for k, e in enumerate(group):
+            for k, e in reversed(list(enumerate(group))):
                 words = h_of[e][:].rearrange("c u p v -> c (u p v)").bitcast(F32)
                 for u in range(2):
                     nc.tensor.transpose(turned[:, k, u, :], words[:, u * P : (u + 1) * P], ident[:])
@@ -192,10 +196,8 @@ def tile_moe_tk_glu_relu_kernel(
             h_codes, h_scales = h_mx[e]
             group = [g for g in Y_GROUPS if e in g][0]
             if e == group[0]:
-                if Y_GROUPS.index(group) < Y_BANKS:
-                    y_of[e] = psum.tile([N, len(group) * C], F32, name="y", bufs=Y_BANKS)
-                else:
-                    y_of[e] = psum.tile([N, len(group) * C], F32, name="y_late", tag="a", bufs=A_BANKS)
+                tag, bufs = Y_PLACES[Y_GROUPS.index(group)]
+                y_of[e] = psum.tile([N, len(group) * C], F32, name="y", tag=tag, bufs=bufs)
             y = y_of[group[0]]
             nc.tensor.matmul_mx(
                 out=y[:, (e - group[0]) * C : (e - group[0] + 1) * C],
@@ -207,7 +209,7 @@ def tile_moe_tk_glu_relu_kernel(
                 stop=True,
             )
             if e == group[-1]:
-                empty = nc.vector.tensor_copy if Y_GROUPS.index(group) % 2 else nc.scalar.copy
+                empty = nc.vector.tensor_copy if Y_GROUPS.index(group) in (2, 4) else nc.scalar.copy
                 empty(y_all[:, group[0] * C : (e + 1) * C], y[:])
 
         for e in range(AHEAD):

@@ -26,13 +26,13 @@ RELU = mybir.ActivationFunctionType.Relu
 LOADS = [(0,), (1, 2), (3, 4, 5), (6, 7), (8, 9), (10, 11)]
 Y_GROUPS = [(0, 1, 2, 3), (4, 5, 6), (7, 8), (9, 10), (11,)]
 TURN_GROUPS = [(0,), (1, 2), (3, 4), (5, 6), (7, 8), (9, 10), (11,)]
-AHEAD = 5
+AHEAD = 3
 LATE = 11
 RANGES = [(0, 6), (6, E)]
-LAG = 3
-LAG2 = 5
-A_BANKS, B_BANKS, TURNED_BANKS, Y_BANKS = 2, 3, 2, 1
-Y_PLACES = [("y", Y_BANKS), ("b", B_BANKS), ("a", A_BANKS), ("a", A_BANKS), ("b", B_BANKS)]
+LAG = 2
+LAG2 = 4
+A_BANKS, B_BANKS, TURNED_BANKS, Y_BANKS = 2, 2, 2, 2
+Y_PLACES = [("y", Y_BANKS), ("y", Y_BANKS), ("y", Y_BANKS), ("a", A_BANKS), ("b", B_BANKS)]
 X_TILE = 256
 X_VECTOR = 160
 W2_EARLY = 6
@@ -116,8 +116,11 @@ def tile_moe_tk_glu_relu_kernel(
             places = held.tile([P, T // 16], U16, name=f"pos_sb_{r}")
             nc.sync.dma_start(places[:], pos)
             pos_sb.append(places)
-        gate_sb = held.tile([P, TOP, T], F32, name="gate_sb")
-        nc.sync.dma_start(gate_sb[:], gate.rearrange("r n t -> n r t"))
+        gate_sb = []
+        for r in range(TOP):
+            weights = held.tile([N, T], F32, name=f"gate_sb_{r}")
+            nc.sync.dma_start(weights[:], gate[r])
+            gate_sb.append(weights)
 
         x_bf16 = [held.tile([P, X_TILE, PACK], BF16, name=f"x_bf16_{i}", align_bytes=64) for i in range(T // X_TILE)]
         for rounded, chunk in zip(x_bf16, x_f32):
@@ -134,12 +137,16 @@ def tile_moe_tk_glu_relu_kernel(
 
         codes_of, scales_of = {}, {}
 
-        def gather(e):
-            listed = offs_sb[:, e * C // 16 : (e + 1) * C // 16]
-            codes_of[e] = gathered.tile([P, C], U32, name="codes", align_bytes=64)
-            scales_of[e] = gathered.tile([P, C], U8, name="scales", align_bytes=64)
-            nc.vector.tensor_copy(codes_of[e][:], x_words[:].indirect(listed))
-            nc.vector.tensor_copy(scales_of[e][:], x_scales[:].indirect(listed))
+        def gather(group):
+            e0, n = group[0], len(group)
+            listed = offs_sb[:, e0 * C // 16 : (e0 + n) * C // 16]
+            codes = gathered.tile([P, n * C], U32, name="codes", align_bytes=64)
+            scales = gathered.tile([P, n * C], U8, name="scales", align_bytes=64)
+            nc.vector.tensor_copy(codes[:], x_words[:].indirect(listed))
+            nc.vector.tensor_copy(scales[:], x_scales[:].indirect(listed))
+            for k, e in enumerate(group):
+                codes_of[e] = codes[:, k * C : (k + 1) * C]
+                scales_of[e] = scales[:, k * C : (k + 1) * C]
 
         def by_pairs(acc):
             return acc.rearrange("c (p u v) -> c u p v", u=2, v=2)
@@ -153,8 +160,8 @@ def tile_moe_tk_glu_relu_kernel(
             for acc, w, s in ((a, w1_sb, s1), (b, w3_sb, s3)):
                 nc.tensor.matmul_mx(
                     out=acc[:],
-                    lhsT=codes_of[e][:].bitcast(FP8X4),
-                    lhsT_scale=scales_of[e][:],
+                    lhsT=codes_of[e].bitcast(FP8X4),
+                    lhsT_scale=scales_of[e],
                     rhs=w[e].bitcast(FP4X4),
                     rhs_scale=s[i][:, e - RANGES[i][0], :],
                     start=True,
@@ -212,8 +219,8 @@ def tile_moe_tk_glu_relu_kernel(
                 empty = nc.vector.tensor_copy if Y_GROUPS.index(group) in (2, 4) else nc.scalar.copy
                 empty(y_all[:, group[0] * C : (e + 1) * C], y[:])
 
-        for e in range(AHEAD):
-            gather(e)
+        for group in TURN_GROUPS[:AHEAD]:
+            gather(group)
         for e in range(E + LAG2):
             if e < E:
                 first_layer(e)
@@ -224,8 +231,9 @@ def tile_moe_tk_glu_relu_kernel(
                 if group[-1] + LAG2 == e:
                     for done in group:
                         second_layer(done)
-            if e + AHEAD < E:
-                gather(e + AHEAD)
+            for done, group in zip(TURN_GROUPS, TURN_GROUPS[AHEAD:]):
+                if done[-1] == e:
+                    gather(group)
 
         parts = [held.tile([N, T], F32, name=f"part_{r}") for r in range(TOP)]
         two = held.tile([N, T], F32, name="two")
@@ -233,7 +241,7 @@ def tile_moe_tk_glu_relu_kernel(
 
         def fetch(r, t0, t1):
             listed = pos_sb[r][:, t0 // 16 : t1 // 16]
-            nc.vector.tensor_tensor(parts[r][:, t0:t1], y_all[:].indirect(listed), gate_sb[:, r, t0:t1], MULT)
+            nc.vector.tensor_tensor(parts[r][:, t0:t1], y_all[:].indirect(listed), gate_sb[r][:, t0:t1], MULT)
 
         fetch(0, 0, T)
         fetch(1, 0, T)

@@ -23,19 +23,21 @@ MULT = mybir.AluOpType.mult
 ADD = mybir.AluOpType.add
 RELU = mybir.ActivationFunctionType.Relu
 
-LOADS = [(0,), (1, 2), (3, 4, 5), (6, 7), (8, 9), (10, 11)]
-Y_GROUPS = [(0, 1, 2, 3), (4, 5, 6), (7, 8), (9, 10), (11,)]
-TURN_GROUPS = [(0,), (1, 2), (3, 4), (5, 6), (7, 8), (9, 10), (11,)]
-AHEAD = 3
-LATE = 11
-RANGES = [(0, 6), (6, E)]
-LAG = 2
-LAG2 = 4
-A_BANKS, B_BANKS, TURNED_BANKS, Y_BANKS = 2, 2, 2, 2
-Y_PLACES = [("y", Y_BANKS), ("y", Y_BANKS), ("y", Y_BANKS), ("a", A_BANKS), ("b", B_BANKS)]
+GROUPS = [(0,)] + [(e, e + 1) for e in range(1, E - 1, 2)] + [(E - 1,)]
+HELD_GROUPS = 3
+TURN_LAG = 2
+SECOND_LAG = 4
+
+SCALE_RANGES = [(0, E // 2), (E // 2, E)]
+EARLY_LOADS = [(0,), (1, 2), (3, 4, 5)]
+LATE_LOADS = [(e, e + 1) for e in range(E // 2, E, 2)]
+
+BANKS = 2
+Y_TILES = [((0, 1, 2), "y"), ((3, 4, 5, 6), "y"), ((7, 8), "b"), ((9, 10, 11), "a")]
+W2_EARLY = 7
+
 X_TILE = 256
 X_VECTOR = 160
-W2_EARLY = 6
 CUT = 384
 
 
@@ -45,29 +47,29 @@ def tile_moe_tk_glu_relu_kernel(
     nc = tc.nc
     with ExitStack() as ctx:
         held = ctx.enter_context(tc.tile_pool(name="held", bufs=1))
-        gathered = ctx.enter_context(tc.tile_pool(name="gathered", bufs=AHEAD))
+        gathered = ctx.enter_context(tc.tile_pool(name="gathered", bufs=HELD_GROUPS))
         products = ctx.enter_context(tc.tile_pool(name="products", bufs=E))
-        hidden = ctx.enter_context(tc.tile_pool(name="hidden", bufs=len(TURN_GROUPS)))
-        psum = ctx.enter_context(tc.psum_pool(name="psum", bufs=1))
+        hidden = ctx.enter_context(tc.tile_pool(name="hidden", bufs=len(GROUPS)))
+        psum = ctx.enter_context(tc.psum_pool(name="psum", bufs=BANKS))
 
-        s1 = [held.tile([P, e1 - e0, H], U8, name=f"s1_{e0}", align_bytes=64) for e0, e1 in RANGES]
-        s3 = [held.tile([P, e1 - e0, H], U8, name=f"s3_{e0}", align_bytes=64) for e0, e1 in RANGES]
+        s1 = [held.tile([P, e1 - e0, H], U8, name=f"s1_{e0}", align_bytes=64) for e0, e1 in SCALE_RANGES]
+        s3 = [held.tile([P, e1 - e0, H], U8, name=f"s3_{e0}", align_bytes=64) for e0, e1 in SCALE_RANGES]
         s2 = held.tile([P, E, N], U8, name="s2", align_bytes=64)
         x_words = held.tile([P, T], U32, name="x_words", align_bytes=64)
         x_scales = held.tile([P, T], U8, name="x_scales", align_bytes=64)
         ident = held.tile([P, P], F32, name="ident")
 
-        def words_of(scales):
+        def as_int32(scales):
             return scales[:].rearrange("p e i -> p (e i)").bitcast(I32)
 
         for scales in (s1[0], s3[0]):
-            half = words_of(scales).shape[1] // 2
-            nc.gpsimd.memset(words_of(scales)[:, :half], 0)
-            nc.vector.memset(words_of(scales)[:, half:], 0)
-        nc.vector.memset(words_of(s2), 0)
+            half = as_int32(scales).shape[1] // 2
+            nc.gpsimd.memset(as_int32(scales)[:, :half], 0)
+            nc.vector.memset(as_int32(scales)[:, half:], 0)
+        nc.vector.memset(as_int32(s2), 0)
         nc.gpsimd.memset(x_scales[:], 0)
-        nc.vector.memset(words_of(s1[1]), 0)
-        nc.vector.memset(words_of(s3[1]), 0)
+        nc.vector.memset(as_int32(s1[1]), 0)
+        nc.vector.memset(as_int32(s3[1]), 0)
         make_identity(nc, ident[:])
 
         x_rows = xT.rearrange("(p j) t -> p j t", j=PACK)
@@ -97,20 +99,21 @@ def tile_moe_tk_glu_relu_kernel(
             load_words("w1", w1_words, w1_sb, H, experts)
             load_words("w3", w3_words, w3_sb, H, experts)
 
-        load_words("w1", w1_words, w1_sb, H, LOADS[0])
-        load_scales(s1[0], w1_scales, *RANGES[0])
-        load_words("w3", w3_words, w3_sb, H, LOADS[0])
-        load_scales(s3[0], w3_scales, *RANGES[0])
-        load_first_layer(LOADS[1])
-        load_first_layer(LOADS[2])
-        load_scales(s1[1], w1_scales, *RANGES[1])
-        load_words("w1", w1_words, w1_sb, H, LOADS[3])
-        load_scales(s3[1], w3_scales, *RANGES[1])
-        load_words("w3", w3_words, w3_sb, H, LOADS[3])
-        for experts in LOADS[4:]:
+        load_words("w1", w1_words, w1_sb, H, EARLY_LOADS[0])
+        load_scales(s1[0], w1_scales, *SCALE_RANGES[0])
+        load_words("w3", w3_words, w3_sb, H, EARLY_LOADS[0])
+        load_scales(s3[0], w3_scales, *SCALE_RANGES[0])
+        for experts in EARLY_LOADS[1:]:
+            load_first_layer(experts)
+        load_scales(s1[1], w1_scales, *SCALE_RANGES[1])
+        load_words("w1", w1_words, w1_sb, H, LATE_LOADS[0])
+        load_scales(s3[1], w3_scales, *SCALE_RANGES[1])
+        load_words("w3", w3_words, w3_sb, H, LATE_LOADS[0])
+        for experts in LATE_LOADS[1:]:
             load_first_layer(experts)
         load_scales(s2, w2_scales, 0, E)
-        load_words("w2", w2_words, w2_sb, N, range(E))
+        load_words("w2", w2_words, w2_sb, N, range(W2_EARLY))
+        load_words("w2", w2_words, w2_sb, N, range(W2_EARLY, E))
         pos_sb = []
         for r, pos in enumerate((pos1, pos2, pos3)):
             places = held.tile([P, T // 16], U16, name=f"pos_sb_{r}")
@@ -154,16 +157,16 @@ def tile_moe_tk_glu_relu_kernel(
         h_of = {}
 
         def first_layer(e):
-            a = psum.tile([C, H], F32, name="a", bufs=A_BANKS)
-            b = psum.tile([C, H], F32, name="b", bufs=B_BANKS)
-            i = [e0 <= e < e1 for e0, e1 in RANGES].index(True)
+            a = psum.tile([C, H], F32, name="a")
+            b = psum.tile([C, H], F32, name="b")
+            part = [e0 <= e < e1 for e0, e1 in SCALE_RANGES].index(True)
             for acc, w, s in ((a, w1_sb, s1), (b, w3_sb, s3)):
                 nc.tensor.matmul_mx(
                     out=acc[:],
                     lhsT=codes_of[e].bitcast(FP8X4),
                     lhsT_scale=scales_of[e],
                     rhs=w[e].bitcast(FP4X4),
-                    rhs_scale=s[i][:, e - RANGES[i][0], :],
+                    rhs_scale=s[part][:, e - SCALE_RANGES[part][0], :],
                     start=True,
                     stop=True,
                 )
@@ -174,19 +177,18 @@ def tile_moe_tk_glu_relu_kernel(
             h_of[e] = h
 
         y_all = held.tile([N, S], F32, name="y_all")
-        y_of = {}
-
+        y_banks = {}
         h_mx = {}
 
         def turn_and_quantise(group):
             n = len(group)
-            turned = psum.tile([P, n, 2, C], F32, name="turned", bufs=TURNED_BANKS)
+            turned = psum.tile([P, n, 2, C], F32, name="turned")
             for k, e in reversed(list(enumerate(group))):
                 words = h_of[e][:].rearrange("c u p v -> c (u p v)").bitcast(F32)
                 for u in range(2):
                     nc.tensor.transpose(turned[:, k, u, :], words[:, u * P : (u + 1) * P], ident[:])
             h_rows = hidden.tile([P, n, C, PACK], BF16, name="h_rows", align_bytes=64)
-            empty = nc.vector.tensor_copy if group[0] >= LATE else nc.scalar.copy
+            empty = nc.vector.tensor_copy if group == GROUPS[-1] else nc.scalar.copy
             empty(h_rows[:].bitcast(F32), turned[:].rearrange("p k u c -> p k c u"))
 
             h_codes = hidden.tile([P, n * C], U32, name="h_codes", align_bytes=64)
@@ -201,13 +203,12 @@ def tile_moe_tk_glu_relu_kernel(
 
         def second_layer(e):
             h_codes, h_scales = h_mx[e]
-            group = [g for g in Y_GROUPS if e in g][0]
-            if e == group[0]:
-                tag, bufs = Y_PLACES[Y_GROUPS.index(group)]
-                y_of[e] = psum.tile([N, len(group) * C], F32, name="y", tag=tag, bufs=bufs)
-            y = y_of[group[0]]
+            sharing, tag = [tile for tile in Y_TILES if e in tile[0]][0]
+            if e == sharing[0]:
+                y_banks[sharing] = psum.tile([N, len(sharing) * C], F32, name="y", tag=tag)
+            y = y_banks[sharing]
             nc.tensor.matmul_mx(
-                out=y[:, (e - group[0]) * C : (e - group[0] + 1) * C],
+                out=y[:, (e - sharing[0]) * C : (e - sharing[0] + 1) * C],
                 lhsT=w2_sb[e].bitcast(FP4X4),
                 lhsT_scale=s2[:, e, :],
                 rhs=h_codes.bitcast(FP8X4),
@@ -215,24 +216,24 @@ def tile_moe_tk_glu_relu_kernel(
                 start=True,
                 stop=True,
             )
-            if e == group[-1]:
-                empty = nc.vector.tensor_copy if Y_GROUPS.index(group) in (2, 4) else nc.scalar.copy
-                empty(y_all[:, group[0] * C : (e + 1) * C], y[:])
+            if e == sharing[-1]:
+                empty = nc.vector.tensor_copy if e == E - 1 else nc.scalar.copy
+                empty(y_all[:, sharing[0] * C : (e + 1) * C], y[:])
 
-        for group in TURN_GROUPS[:AHEAD]:
+        for group in GROUPS[:HELD_GROUPS]:
             gather(group)
-        for e in range(E + LAG2):
-            if e < E:
-                first_layer(e)
-            for group in TURN_GROUPS:
-                if group[-1] + LAG == e:
+        for step in range(E + SECOND_LAG):
+            if step < E:
+                first_layer(step)
+            for group in GROUPS:
+                if group[-1] + TURN_LAG == step:
                     turn_and_quantise(group)
-            for group in TURN_GROUPS:
-                if group[-1] + LAG2 == e:
-                    for done in group:
-                        second_layer(done)
-            for done, group in zip(TURN_GROUPS, TURN_GROUPS[AHEAD:]):
-                if done[-1] == e:
+            for group in GROUPS:
+                if group[-1] + SECOND_LAG == step:
+                    for e in group:
+                        second_layer(e)
+            for ended, group in zip(GROUPS, GROUPS[HELD_GROUPS:]):
+                if ended[-1] == step:
                     gather(group)
 
         parts = [held.tile([N, T], F32, name=f"part_{r}") for r in range(TOP)]

@@ -23,21 +23,14 @@ MULT = mybir.AluOpType.mult
 ADD = mybir.AluOpType.add
 RELU = mybir.ActivationFunctionType.Relu
 
-GROUPS = [(0,)] + [(e, e + 1) for e in range(1, E - 1, 2)] + [(E - 1,)]
-HELD_GROUPS = 3
-TURN_LAG = 2
-SECOND_LAG = 4
-
-SCALE_RANGES = [(0, E // 2), (E // 2, E)]
-EARLY_LOADS = [(0,), (1, 2), (3, 4, 5)]
-LATE_LOADS = [(e, e + 1) for e in range(E // 2, E, 2)]
-
-BANKS = 2
-Y_TILES = [((0, 1, 2), "y"), ((3, 4, 5, 6), "y"), ((7, 8), "b"), ((9, 10, 11), "a")]
-W2_EARLY = 7
-
-X_TILE = 256
-X_VECTOR = 160
+GATHERS = [(0,), (1, 2), (3, 4, 5), (6, 7, 8), (9, 10), (11,)]
+GROUPS = [(0, 1), (2, 3), (4, 5), (6, 7), (8, 9), (10,), (11,)]
+W1_LOADS = [(0, 1), (2, 3, 4, 5), (6, 7, 8, 9, 10, 11)]
+W3_LOADS = [(0, 1), (2, 3, 4), (5, 6, 7), (8, 9, 10, 11)]
+Y_TILES = [((0, 1, 2, 3), "a", False), ((4, 5, 6, 7), "a", False), ((8, 9), "a", False), ((10, 11), "b", True)]
+TURN_LAG = 1
+QUANT_AT = [12, 12, 12, 12, 13, 14, 15]
+X_TILES = [(256, 160), (256, 160)]
 CUT = 384
 
 
@@ -47,13 +40,11 @@ def tile_moe_tk_glu_relu_kernel(
     nc = tc.nc
     with ExitStack() as ctx:
         held = ctx.enter_context(tc.tile_pool(name="held", bufs=1))
-        gathered = ctx.enter_context(tc.tile_pool(name="gathered", bufs=HELD_GROUPS))
-        products = ctx.enter_context(tc.tile_pool(name="products", bufs=E))
-        hidden = ctx.enter_context(tc.tile_pool(name="hidden", bufs=len(GROUPS)))
-        psum = ctx.enter_context(tc.psum_pool(name="psum", bufs=BANKS))
+        psum = ctx.enter_context(tc.psum_pool(name="psum", bufs=1))
+        banks = {"a": 2, "b": 4, "turned": 2}
 
-        s1 = [held.tile([P, e1 - e0, H], U8, name=f"s1_{e0}", align_bytes=64) for e0, e1 in SCALE_RANGES]
-        s3 = [held.tile([P, e1 - e0, H], U8, name=f"s3_{e0}", align_bytes=64) for e0, e1 in SCALE_RANGES]
+        s1 = held.tile([P, E, H], U8, name="s1", align_bytes=64)
+        s3 = held.tile([P, E, H], U8, name="s3", align_bytes=64)
         s2 = held.tile([P, E, N], U8, name="s2", align_bytes=64)
         x_words = held.tile([P, T], U32, name="x_words", align_bytes=64)
         x_scales = held.tile([P, T], U8, name="x_scales", align_bytes=64)
@@ -62,27 +53,24 @@ def tile_moe_tk_glu_relu_kernel(
         def as_int32(scales):
             return scales[:].rearrange("p e i -> p (e i)").bitcast(I32)
 
-        for scales in (s1[0], s3[0]):
-            half = as_int32(scales).shape[1] // 2
-            nc.gpsimd.memset(as_int32(scales)[:, :half], 0)
-            nc.vector.memset(as_int32(scales)[:, half:], 0)
-        nc.vector.memset(as_int32(s2), 0)
+        for scales in (s1, s3, s2):
+            nc.vector.memset(as_int32(scales), 0)
         nc.gpsimd.memset(x_scales[:], 0)
-        nc.vector.memset(as_int32(s1[1]), 0)
-        nc.vector.memset(as_int32(s3[1]), 0)
         make_identity(nc, ident[:])
 
         x_rows = xT.rearrange("(p j) t -> p j t", j=PACK)
         x_f32 = []
-        for t0 in range(0, T, X_TILE):
-            chunk = held.tile([P, PACK, X_TILE], F32, name=f"x_f32_{t0}")
-            nc.sync.dma_start(chunk[:], x_rows[:, :, t0 : t0 + X_TILE])
-            x_f32.append(chunk)
+        t0 = 0
+        for tokens, by_vector in X_TILES:
+            chunk = held.tile([P, PACK, tokens], F32, name=f"x_f32_{t0}")
+            nc.sync.dma_start(chunk[:], x_rows[:, :, t0 : t0 + tokens])
+            x_f32.append((t0, tokens, by_vector, chunk))
+            t0 = t0 + tokens
         offs_sb = held.tile([P, S // 16], U16, name="offs_sb")
         nc.sync.dma_start(offs_sb[:], offs)
 
-        def load_scales(tile, scales, e0, e1):
-            rows = scales[e0:e1, 0].rearrange("e (q r) i -> r q e i", r=4)
+        def load_scales(tile, scales):
+            rows = scales[:, 0].rearrange("e (q r) i -> r q e i", r=4)
             for r in range(4):
                 nc.sync.dma_start(tile[r:P:32, :, :].bitcast(I32), rows[r].bitcast(I32))
 
@@ -95,25 +83,18 @@ def tile_moe_tk_glu_relu_kernel(
             for k in range(n):
                 by_expert[e0 + k] = w[:, k, :]
 
-        def load_first_layer(experts):
-            load_words("w1", w1_words, w1_sb, H, experts)
-            load_words("w3", w3_words, w3_sb, H, experts)
-
-        load_words("w1", w1_words, w1_sb, H, EARLY_LOADS[0])
-        load_scales(s1[0], w1_scales, *SCALE_RANGES[0])
-        load_words("w3", w3_words, w3_sb, H, EARLY_LOADS[0])
-        load_scales(s3[0], w3_scales, *SCALE_RANGES[0])
-        for experts in EARLY_LOADS[1:]:
-            load_first_layer(experts)
-        load_scales(s1[1], w1_scales, *SCALE_RANGES[1])
-        load_words("w1", w1_words, w1_sb, H, LATE_LOADS[0])
-        load_scales(s3[1], w3_scales, *SCALE_RANGES[1])
-        load_words("w3", w3_words, w3_sb, H, LATE_LOADS[0])
-        for experts in LATE_LOADS[1:]:
-            load_first_layer(experts)
-        load_scales(s2, w2_scales, 0, E)
-        load_words("w2", w2_words, w2_sb, N, range(W2_EARLY))
-        load_words("w2", w2_words, w2_sb, N, range(W2_EARLY, E))
+        load_scales(s1, w1_scales)
+        load_words("w1", w1_words, w1_sb, H, (0, 1))
+        load_words("w1", w1_words, w1_sb, H, (2, 3, 4, 5))
+        load_words("w1", w1_words, w1_sb, H, (6, 7, 8))
+        load_scales(s2, w2_scales)
+        load_scales(s3, w3_scales)
+        load_words("w3", w3_words, w3_sb, H, (0, 1, 2, 3))
+        load_words("w1", w1_words, w1_sb, H, (9, 10, 11))
+        load_words("w3", w3_words, w3_sb, H, (4, 5))
+        load_words("w3", w3_words, w3_sb, H, (6, 7, 8))
+        load_words("w2", w2_words, w2_sb, N, range(E))
+        load_words("w3", w3_words, w3_sb, H, (9, 10, 11))
         pos_sb = []
         for r, pos in enumerate((pos1, pos2, pos3)):
             places = held.tile([P, T // 16], U16, name=f"pos_sb_{r}")
@@ -125,16 +106,17 @@ def tile_moe_tk_glu_relu_kernel(
             nc.sync.dma_start(weights[:], gate[r])
             gate_sb.append(weights)
 
-        x_bf16 = [held.tile([P, X_TILE, PACK], BF16, name=f"x_bf16_{i}", align_bytes=64) for i in range(T // X_TILE)]
-        for rounded, chunk in zip(x_bf16, x_f32):
+        x_bf16 = []
+        for t0, tokens, by_vector, chunk in x_f32:
+            rounded = held.tile([P, tokens, PACK], BF16, name=f"x_bf16_{t0}", align_bytes=64)
             rows = chunk[:].rearrange("p j t -> p t j")
-            nc.vector.tensor_copy(rounded[:, :X_VECTOR, :], rows[:, :X_VECTOR, :])
-            nc.scalar.copy(rounded[:, X_VECTOR:, :], rows[:, X_VECTOR:, :])
-        for i, rounded in enumerate(x_bf16):
-            cols = slice(X_TILE * i, X_TILE * (i + 1))
+            nc.vector.tensor_copy(rounded[:, :by_vector, :], rows[:, :by_vector, :])
+            nc.scalar.copy(rounded[:, by_vector:, :], rows[:, by_vector:, :])
+            x_bf16.append((t0, tokens, rounded))
+        for t0, tokens, rounded in x_bf16:
             nc.vector.quantize_mx(
-                out=x_words[:, cols].bitcast(FP8X4),
-                scales=x_scales[:, cols],
+                out=x_words[:, t0 : t0 + tokens].bitcast(FP8X4),
+                scales=x_scales[:, t0 : t0 + tokens],
                 in_=rounded[:].rearrange("p t j -> p (t j)"),
             )
 
@@ -143,8 +125,8 @@ def tile_moe_tk_glu_relu_kernel(
         def gather(group):
             e0, n = group[0], len(group)
             listed = offs_sb[:, e0 * C // 16 : (e0 + n) * C // 16]
-            codes = gathered.tile([P, n * C], U32, name="codes", align_bytes=64)
-            scales = gathered.tile([P, n * C], U8, name="scales", align_bytes=64)
+            codes = held.tile([P, n * C], U32, name=f"codes_{e0}", align_bytes=64)
+            scales = held.tile([P, n * C], U8, name=f"scales_{e0}", align_bytes=64)
             nc.vector.tensor_copy(codes[:], x_words[:].indirect(listed))
             nc.vector.tensor_copy(scales[:], x_scales[:].indirect(listed))
             for k, e in enumerate(group):
@@ -154,87 +136,95 @@ def tile_moe_tk_glu_relu_kernel(
         def by_pairs(acc):
             return acc.rearrange("c (p u v) -> c u p v", u=2, v=2)
 
-        h_of = {}
+        def first_layer(e, tag, w, s):
+            acc = psum.tile([C, H], F32, name="acc", tag=tag, bufs=banks[tag])
+            nc.tensor.matmul_mx(
+                out=acc[:],
+                lhsT=codes_of[e].bitcast(FP8X4),
+                lhsT_scale=scales_of[e],
+                rhs=w[e].bitcast(FP4X4),
+                rhs_scale=s[:, e, :],
+                start=True,
+                stop=True,
+            )
+            return acc
 
-        def first_layer(e):
-            a = psum.tile([C, H], F32, name="a")
-            b = psum.tile([C, H], F32, name="b")
-            part = [e0 <= e < e1 for e0, e1 in SCALE_RANGES].index(True)
-            for acc, w, s in ((a, w1_sb, s1), (b, w3_sb, s3)):
-                nc.tensor.matmul_mx(
-                    out=acc[:],
-                    lhsT=codes_of[e].bitcast(FP8X4),
-                    lhsT_scale=scales_of[e],
-                    rhs=w[e].bitcast(FP4X4),
-                    rhs_scale=s[part][:, e - SCALE_RANGES[part][0], :],
-                    start=True,
-                    stop=True,
-                )
-            relu_a = products.tile([C, 2, P, 2], F32, name="relu_a")
+        relu_of, h_of = {}, {}
+
+        def gate_half(e):
+            a = first_layer(e, ("turned" if e % 2 == 1 else "a") if e < 9 else ("turned" if e == 10 else "a"), w1_sb, s1)
+            relu_a = held.tile([C, 2, P, 2], F32, name=f"relu_a_{e}", tag=f"relu_a_{e}", align_bytes=64)
             nc.scalar.activation(relu_a[:], by_pairs(a[:]), RELU)
-            h = products.tile([C, 2, P, 2], BF16, name="h")
-            nc.vector.tensor_tensor(h[:], by_pairs(b[:]), relu_a[:], MULT)
+            relu_of[e] = relu_a
+
+        def product(e):
+            b = first_layer(e, "b", w3_sb, s3)
+            h = held.tile([C, 2, P, 2], BF16, name=f"h_{e}")
+            nc.vector.tensor_tensor(h[:], by_pairs(b[:]), relu_of[e][:], MULT)
             h_of[e] = h
 
         y_all = held.tile([N, S], F32, name="y_all")
         y_banks = {}
-        h_mx = {}
+        rows_of = {}
+        late = []
 
-        def turn_and_quantise(group):
+        def turn(group):
             n = len(group)
-            turned = psum.tile([P, n, 2, C], F32, name="turned")
+            turned = psum.tile([P, n, 2, C], F32, name="turned", tag="turned", bufs=banks["turned"])
             for k, e in reversed(list(enumerate(group))):
                 words = h_of[e][:].rearrange("c u p v -> c (u p v)").bitcast(F32)
                 for u in range(2):
                     nc.tensor.transpose(turned[:, k, u, :], words[:, u * P : (u + 1) * P], ident[:])
-            h_rows = hidden.tile([P, n, C, PACK], BF16, name="h_rows", align_bytes=64)
-            empty = nc.vector.tensor_copy if group == GROUPS[-1] else nc.scalar.copy
+            h_rows = held.tile([P, n, C, PACK], BF16, name=f"h_rows_{group[0]}", align_bytes=64)
+            empty = nc.vector.tensor_copy if group in () else nc.scalar.copy
             empty(h_rows[:].bitcast(F32), turned[:].rearrange("p k u c -> p k c u"))
+            rows_of[group] = h_rows
 
-            h_codes = hidden.tile([P, n * C], U32, name="h_codes", align_bytes=64)
-            h_scales = hidden.tile([P, n * C], U8, name="h_scales", align_bytes=64)
+        def second_layer(group):
+            n = len(group)
+            if group[0] < 0 or group[0] > 10:
+                h_codes = held.tile([P, n * C], U32, name=f"h_codes_{group[0]}", align_bytes=64)
+            else:
+                if not late:
+                    late.append(held.tile([P, 11 * C], U32, name="late", tag="relu_a_10", align_bytes=64))
+                h_codes = late[0][:, (group[0] - 0) * C : (group[-1] + 1 - 0) * C]
+            h_scales = held.tile([P, n * C], U8, name=f"h_scales_{group[0]}", align_bytes=64)
             nc.vector.quantize_mx(
                 out=h_codes[:].bitcast(FP8X4),
                 scales=h_scales[:],
-                in_=h_rows[:].rearrange("p k c j -> p (k c j)"),
+                in_=rows_of[group][:].rearrange("p k c j -> p (k c j)"),
             )
             for k, e in enumerate(group):
-                h_mx[e] = (h_codes[:, k * C : (k + 1) * C], h_scales[:, k * C : (k + 1) * C])
+                sharing, tag, by_vector = [tile for tile in Y_TILES if e in tile[0]][0]
+                if e == sharing[0]:
+                    y_banks[sharing] = psum.tile([N, len(sharing) * C], F32, name="y", tag=tag, bufs=banks[tag])
+                y = y_banks[sharing]
+                nc.tensor.matmul_mx(
+                    out=y[:, (e - sharing[0]) * C : (e - sharing[0] + 1) * C],
+                    lhsT=w2_sb[e].bitcast(FP4X4),
+                    lhsT_scale=s2[:, e, :],
+                    rhs=h_codes[:, k * C : (k + 1) * C].bitcast(FP8X4),
+                    rhs_scale=h_scales[:, k * C : (k + 1) * C],
+                    start=True,
+                    stop=True,
+                )
+                if e == sharing[-1]:
+                    empty = nc.vector.tensor_copy if by_vector else nc.scalar.copy
+                    empty(y_all[:, sharing[0] * C : (e + 1) * C], y[:])
 
-        def second_layer(e):
-            h_codes, h_scales = h_mx[e]
-            sharing, tag = [tile for tile in Y_TILES if e in tile[0]][0]
-            if e == sharing[0]:
-                y_banks[sharing] = psum.tile([N, len(sharing) * C], F32, name="y", tag=tag)
-            y = y_banks[sharing]
-            nc.tensor.matmul_mx(
-                out=y[:, (e - sharing[0]) * C : (e - sharing[0] + 1) * C],
-                lhsT=w2_sb[e].bitcast(FP4X4),
-                lhsT_scale=s2[:, e, :],
-                rhs=h_codes.bitcast(FP8X4),
-                rhs_scale=h_scales,
-                start=True,
-                stop=True,
-            )
-            if e == sharing[-1]:
-                empty = nc.vector.tensor_copy if e == E - 1 else nc.scalar.copy
-                empty(y_all[:, sharing[0] * C : (e + 1) * C], y[:])
-
-        for group in GROUPS[:HELD_GROUPS]:
+        for group in GATHERS:
             gather(group)
-        for step in range(E + SECOND_LAG):
+        for e in range(E):
+            gate_half(e)
+        for step in range(E + 8):
             if step < E:
-                first_layer(step)
+                product(step)
             for group in GROUPS:
                 if group[-1] + TURN_LAG == step:
-                    turn_and_quantise(group)
-            for group in GROUPS:
-                if group[-1] + SECOND_LAG == step:
-                    for e in group:
-                        second_layer(e)
-            for ended, group in zip(GROUPS, GROUPS[HELD_GROUPS:]):
-                if ended[-1] == step:
-                    gather(group)
+                    turn(group)
+            for group, at in zip(GROUPS, QUANT_AT):
+                if at == step:
+                    second_layer(group)
 
         parts = [held.tile([N, T], F32, name=f"part_{r}") for r in range(TOP)]
         two = held.tile([N, T], F32, name="two")

@@ -23,13 +23,14 @@ MULT = mybir.AluOpType.mult
 ADD = mybir.AluOpType.add
 RELU = mybir.ActivationFunctionType.Relu
 
+BANK = 2048
 GATHERS = [(0,), (1, 2), (3, 4, 5), (6, 7, 8), (9, 10), (11,)]
 GROUPS = [(0, 1), (2, 3), (4, 5), (6, 7), (8, 9), (10,), (11,)]
-W1_LOADS = [(0, 1), (2, 3, 4, 5), (6, 7, 8, 9, 10, 11)]
-W3_LOADS = [(0, 1), (2, 3, 4), (5, 6, 7), (8, 9, 10, 11)]
-Y_TILES = [((0, 1, 2, 3), "a", False), ((4, 5, 6, 7), "a", False), ((8, 9), "a", False), ((10, 11), "b", True)]
-TURN_LAG = 1
-QUANT_AT = [12, 12, 12, 12, 13, 14, 15]
+RANGES = [(0, 6), (6, 12)]
+A_BANK = [0, 1, 2, 3, 0, 1, 2, 3, 7, 6, 0, 1]
+B_BANK = [4, 5, 6, 0, 1, 2, 4, 5, 2, 3, 7, 6]
+T_BANK = [3, 7, 4, 5, 0, 1, 2]
+Y_TILES = [((0, 1, 2, 3), 3, False), ((4, 5, 6, 7), 4, False), ((8, 9), 5, True), ((10, 11), 7, True)]
 X_TILES = [(256, 160), (256, 160)]
 CUT = 384
 
@@ -41,19 +42,17 @@ def tile_moe_tk_glu_relu_kernel(
     with ExitStack() as ctx:
         held = ctx.enter_context(tc.tile_pool(name="held", bufs=1))
         psum = ctx.enter_context(tc.psum_pool(name="psum", bufs=1))
-        banks = {"a": 2, "b": 4, "turned": 2}
 
-        s1 = held.tile([P, E, H], U8, name="s1", align_bytes=64)
-        s3 = held.tile([P, E, H], U8, name="s3", align_bytes=64)
-        s2 = held.tile([P, E, N], U8, name="s2", align_bytes=64)
-        x_words = held.tile([P, T], U32, name="x_words", align_bytes=64)
+        s1 = [held.tile([P, e1 - e0, H], U8, name=f"s1_{e0}", align_bytes=64) for e0, e1 in RANGES]
+        s3 = [held.tile([P, e1 - e0, H], U8, name=f"s3_{e0}", align_bytes=64) for e0, e1 in RANGES]
+        x_words = held.tile([P, T], U32, name="x_words", tag="x_words", align_bytes=64)
         x_scales = held.tile([P, T], U8, name="x_scales", align_bytes=64)
         ident = held.tile([P, P], F32, name="ident")
 
         def as_int32(scales):
             return scales[:].rearrange("p e i -> p (e i)").bitcast(I32)
 
-        for scales in (s1, s3, s2):
+        for scales in (s1[0], s1[1], s3[0], s3[1]):
             nc.vector.memset(as_int32(scales), 0)
         nc.gpsimd.memset(x_scales[:], 0)
         make_identity(nc, ident[:])
@@ -69,32 +68,44 @@ def tile_moe_tk_glu_relu_kernel(
         offs_sb = held.tile([P, S // 16], U16, name="offs_sb")
         nc.sync.dma_start(offs_sb[:], offs)
 
-        def load_scales(tile, scales):
-            rows = scales[:, 0].rearrange("e (q r) i -> r q e i", r=4)
+        def load_scales(tile, scales, e0, e1, queue=nc.sync):
+            rows = scales[e0:e1, 0].rearrange("e (q r) i -> r q e i", r=4)
             for r in range(4):
-                nc.sync.dma_start(tile[r:P:32, :, :].bitcast(I32), rows[r].bitcast(I32))
+                queue.dma_start(tile[r:P:32, :, :].bitcast(I32), rows[r].bitcast(I32))
 
         w1_sb, w3_sb, w2_sb = {}, {}, {}
 
         def load_words(name, words, by_expert, width, experts):
             e0, n = experts[0], len(experts)
-            w = held.tile([P, n, 2 * width], U8, name=f"{name}_{e0}", align_bytes=64)
+            w = held.tile([P, n, 2 * width], U8, name=f"{name}_{e0}", tag=f"{name}_{e0}", align_bytes=64)
             nc.sync.dma_start(w[:].bitcast(I32), words[e0 : e0 + n, 0].rearrange("e p b -> p e b").bitcast(I32))
             for k in range(n):
                 by_expert[e0 + k] = w[:, k, :]
 
-        load_scales(s1, w1_scales)
-        load_words("w1", w1_words, w1_sb, H, (0, 1))
-        load_words("w1", w1_words, w1_sb, H, (2, 3, 4, 5))
-        load_words("w1", w1_words, w1_sb, H, (6, 7, 8))
-        load_scales(s2, w2_scales)
-        load_scales(s3, w3_scales)
-        load_words("w3", w3_words, w3_sb, H, (0, 1, 2, 3))
-        load_words("w1", w1_words, w1_sb, H, (9, 10, 11))
-        load_words("w3", w3_words, w3_sb, H, (4, 5))
-        load_words("w3", w3_words, w3_sb, H, (6, 7, 8))
-        load_words("w2", w2_words, w2_sb, N, range(E))
-        load_words("w3", w3_words, w3_sb, H, (9, 10, 11))
+        def w1(*experts):
+            load_words("w1", w1_words, w1_sb, H, experts)
+
+        def w3(*experts):
+            load_words("w3", w3_words, w3_sb, H, experts)
+
+        def w2(*experts):
+            load_words("w2", w2_words, w2_sb, N, experts)
+
+        load_scales(s1[0], w1_scales, *RANGES[0])
+        w1(0, 1)
+        w1(2, 3, 4, 5)
+        load_scales(s1[1], w1_scales, *RANGES[1])
+        w1(6, 7, 8)
+        load_scales(s3[0], w3_scales, *RANGES[0])
+        w3(0, 1, 2)
+        w3(3, 4, 5)
+        load_scales(s3[1], w3_scales, *RANGES[1])
+        w3(6, 7)
+        w1(9, 10, 11)
+        w3(8, 9)
+        w3(10, 11)
+        w2(0, 1, 2, 3, 4, 5, 6, 7)
+        w2(8, 9, 10, 11)
         pos_sb = []
         for r, pos in enumerate((pos1, pos2, pos3)):
             places = held.tile([P, T // 16], U16, name=f"pos_sb_{r}")
@@ -136,95 +147,124 @@ def tile_moe_tk_glu_relu_kernel(
         def by_pairs(acc):
             return acc.rearrange("c (p u v) -> c u p v", u=2, v=2)
 
-        def first_layer(e, tag, w, s):
-            acc = psum.tile([C, H], F32, name="acc", tag=tag, bufs=banks[tag])
+        def first_layer(e, name, bank, w, s):
+            acc = psum.tile([C, H], F32, name=f"{name}_{e}", offset=bank * BANK)
+            part = [e0 <= e < e1 for e0, e1 in RANGES].index(True)
             nc.tensor.matmul_mx(
                 out=acc[:],
                 lhsT=codes_of[e].bitcast(FP8X4),
                 lhsT_scale=scales_of[e],
                 rhs=w[e].bitcast(FP4X4),
-                rhs_scale=s[:, e, :],
+                rhs_scale=s[part][:, e - RANGES[part][0], :],
                 start=True,
                 stop=True,
             )
             return acc
 
-        relu_of, h_of = {}, {}
-
-        def gate_half(e):
-            a = first_layer(e, ("turned" if e % 2 == 1 else "a") if e < 9 else ("turned" if e == 10 else "a"), w1_sb, s1)
-            relu_a = held.tile([C, 2, P, 2], F32, name=f"relu_a_{e}", tag=f"relu_a_{e}", align_bytes=64)
-            nc.scalar.activation(relu_a[:], by_pairs(a[:]), RELU)
-            relu_of[e] = relu_a
-
-        def product(e):
-            b = first_layer(e, "b", w3_sb, s3)
-            h = held.tile([C, 2, P, 2], BF16, name=f"h_{e}")
-            nc.vector.tensor_tensor(h[:], by_pairs(b[:]), relu_of[e][:], MULT)
-            h_of[e] = h
-
+        relu_of, b_of, h_of, rows_of, y_banks = {}, {}, {}, {}, {}
         y_all = held.tile([N, S], F32, name="y_all")
-        y_banks = {}
-        rows_of = {}
-        late = []
 
-        def turn(group):
+        def A(*experts):
+            for e in experts:
+                a = first_layer(e, "a", A_BANK[e], w1_sb, s1)
+                relu_a = held.tile([C, 2, P, 2], F32, name=f"relu_a_{e}", tag=f"relu_a_{e}", align_bytes=64)
+                nc.scalar.activation(relu_a[:], by_pairs(a[:]), RELU)
+                relu_of[e] = relu_a
+
+        def B(*experts):
+            for e in experts:
+                b_of[e] = first_layer(e, "b", B_BANK[e], w3_sb, s3)
+
+        def M(*experts):
+            for e in experts:
+                h = held.tile([C, 2, P, 2], BF16, name=f"h_{e}")
+                nc.vector.tensor_tensor(h[:], by_pairs(b_of[e][:]), relu_of[e][:], MULT)
+                h_of[e] = h
+
+        def G(*experts):
+            for e in experts:
+                h = held.tile([C, 2, P, 2], BF16, name=f"h_{e}")
+                b_sb = held.tile([C, 2, P, 2], F32, name=f"b_sb_{e}")
+                nc.scalar.copy(b_sb[:], by_pairs(b_of[e][:]))
+                nc.gpsimd.tensor_tensor(h[:], b_sb[:], relu_of[e][:], MULT)
+                h_of[e] = h
+
+        def turn(g, empty=nc.scalar.copy):
+            group = GROUPS[g]
             n = len(group)
-            turned = psum.tile([P, n, 2, C], F32, name="turned", tag="turned", bufs=banks["turned"])
+            turned = psum.tile([P, n, 2, C], F32, name=f"turned_{g}", offset=T_BANK[g] * BANK)
             for k, e in reversed(list(enumerate(group))):
                 words = h_of[e][:].rearrange("c u p v -> c (u p v)").bitcast(F32)
                 for u in range(2):
                     nc.tensor.transpose(turned[:, k, u, :], words[:, u * P : (u + 1) * P], ident[:])
-            h_rows = held.tile([P, n, C, PACK], BF16, name=f"h_rows_{group[0]}", align_bytes=64)
-            empty = nc.vector.tensor_copy if group in () else nc.scalar.copy
+            h_rows = held.tile([P, n, C, PACK], BF16, name=f"h_rows_{g}", align_bytes=64)
             empty(h_rows[:].bitcast(F32), turned[:].rearrange("p k u c -> p k c u"))
-            rows_of[group] = h_rows
+            rows_of[g] = h_rows
 
-        def second_layer(group):
+        mx_of = {}
+
+        def Q(g, tag=None):
+            group = GROUPS[g]
             n = len(group)
-            if group[0] < 0 or group[0] > 10:
-                h_codes = held.tile([P, n * C], U32, name=f"h_codes_{group[0]}", align_bytes=64)
-            else:
-                if not late:
-                    late.append(held.tile([P, 11 * C], U32, name="late", tag="relu_a_10", align_bytes=64))
-                h_codes = late[0][:, (group[0] - 0) * C : (group[-1] + 1 - 0) * C]
-            h_scales = held.tile([P, n * C], U8, name=f"h_scales_{group[0]}", align_bytes=64)
+            h_codes = held.tile([P, n * C], U32, name=f"h_codes_{g}", tag=tag or f"h_codes_{g}", align_bytes=64)
+            h_scales = held.tile([P, n * C], U8, name=f"h_scales_{g}", align_bytes=64)
             nc.vector.quantize_mx(
                 out=h_codes[:].bitcast(FP8X4),
                 scales=h_scales[:],
-                in_=rows_of[group][:].rearrange("p k c j -> p (k c j)"),
+                in_=rows_of[g][:].rearrange("p k c j -> p (k c j)"),
             )
             for k, e in enumerate(group):
-                sharing, tag, by_vector = [tile for tile in Y_TILES if e in tile[0]][0]
-                if e == sharing[0]:
-                    y_banks[sharing] = psum.tile([N, len(sharing) * C], F32, name="y", tag=tag, bufs=banks[tag])
-                y = y_banks[sharing]
+                mx_of[e] = (h_codes[:, k * C : (k + 1) * C], h_scales[:, k * C : (k + 1) * C])
+
+        def Y(j):
+            sharing, bank, by_vector = Y_TILES[j]
+            y = psum.tile([N, len(sharing) * C], F32, name=f"y_{j}", offset=bank * BANK)
+            for k, e in enumerate(sharing):
                 nc.tensor.matmul_mx(
-                    out=y[:, (e - sharing[0]) * C : (e - sharing[0] + 1) * C],
+                    out=y[:, k * C : (k + 1) * C],
                     lhsT=w2_sb[e].bitcast(FP4X4),
                     lhsT_scale=s2[:, e, :],
-                    rhs=h_codes[:, k * C : (k + 1) * C].bitcast(FP8X4),
-                    rhs_scale=h_scales[:, k * C : (k + 1) * C],
+                    rhs=mx_of[e][0].bitcast(FP8X4),
+                    rhs_scale=mx_of[e][1],
                     start=True,
                     stop=True,
                 )
-                if e == sharing[-1]:
-                    empty = nc.vector.tensor_copy if by_vector else nc.scalar.copy
-                    empty(y_all[:, sharing[0] * C : (e + 1) * C], y[:])
+            empty = nc.vector.tensor_copy if by_vector else nc.scalar.copy
+            empty(y_all[:, sharing[0] * C : (sharing[-1] + 1) * C], y[:])
 
         for group in GATHERS:
             gather(group)
-        for e in range(E):
-            gate_half(e)
-        for step in range(E + 8):
-            if step < E:
-                product(step)
-            for group in GROUPS:
-                if group[-1] + TURN_LAG == step:
-                    turn(group)
-            for group, at in zip(GROUPS, QUANT_AT):
-                if at == step:
-                    second_layer(group)
+        s2 = held.tile([P, E, N], U8, name="s2", tag="x_words", align_bytes=64)
+        nc.gpsimd.memset(as_int32(s2), 0)
+        load_scales(s2, w2_scales, 0, E, nc.gpsimd)
+        A(0, 1, 2, 3, 4, 5, 6, 7, 8)
+        B(0, 1, 2, 3, 4, 5)
+        M(0, 1)
+        turn(0)
+        M(2, 3)
+        turn(1)
+        B(6, 7)
+        M(4, 5)
+        Q(0)
+        Q(1)
+        A(9, 10, 11)
+        B(8, 9)
+        B(10, 11)
+        M(6)
+        turn(2)
+        M(7)
+        turn(3)
+        M(8, 9)
+        turn(4)
+        Q(2)
+        M(10)
+        turn(5)
+        M(11)
+        turn(6)
+        for g in range(3, 7):
+            Q(g)
+        for j in range(4):
+            Y(j)
 
         parts = [held.tile([N, T], F32, name=f"part_{r}") for r in range(TOP)]
         two = held.tile([N, T], F32, name="two")

@@ -27,10 +27,10 @@ BANK = 2048
 GATHERS = [(0,), (1, 2), (3, 4, 5), (6, 7, 8), (9, 10), (11,)]
 GROUPS = [(0, 1), (2, 3), (4, 5), (6, 7), (8, 9), (10,), (11,)]
 RANGES = [(0, 6), (6, 12)]
-A_BANK = [0, 1, 2, 3, 0, 1, 2, 3, 7, 6, 0, 1]
-B_BANK = [4, 5, 6, 0, 1, 2, 4, 5, 2, 3, 7, 6]
-T_BANK = [3, 7, 4, 5, 0, 1, 2]
-Y_TILES = [((0, 1, 2, 3), 3, False), ((4, 5, 6, 7), 4, False), ((8, 9), 5, True), ((10, 11), 7, True)]
+A_BANK = [0, 1, 2, 3, 0, 1, 2, 3, 2, 7, 0, 1]
+B_BANK = [4, 5, 6, 7, 0, 1, 5, 4, 3, 6, 5, 2]
+T_BANK = [3, 6, 4, 7, 0, 1, 4]
+Y_TILES = [((0, 1, 2, 3), 3, False), ((4, 5, 6, 7), 6, False), ((8, 9), 5, True), ((10, 11), 7, True)]
 X_TILES = [(256, 160), (256, 160)]
 CUT = 384
 
@@ -43,8 +43,8 @@ def tile_moe_tk_glu_relu_kernel(
         held = ctx.enter_context(tc.tile_pool(name="held", bufs=1))
         psum = ctx.enter_context(tc.psum_pool(name="psum", bufs=1))
 
-        s1 = [held.tile([P, e1 - e0, H], U8, name=f"s1_{e0}", align_bytes=64) for e0, e1 in RANGES]
-        s3 = [held.tile([P, e1 - e0, H], U8, name=f"s3_{e0}", align_bytes=64) for e0, e1 in RANGES]
+        s1 = [held.tile([P, E, H], U8, name="s1", align_bytes=64)]
+        s3 = [held.tile([P, RANGES[0][1], H], U8, name="s3_0", align_bytes=64)]
         x_words = held.tile([P, T], U32, name="x_words", tag="x_words", align_bytes=64)
         x_scales = held.tile([P, T], U8, name="x_scales", align_bytes=64)
         ident = held.tile([P, P], F32, name="ident")
@@ -52,7 +52,7 @@ def tile_moe_tk_glu_relu_kernel(
         def as_int32(scales):
             return scales[:].rearrange("p e i -> p (e i)").bitcast(I32)
 
-        for scales in (s1[0], s1[1], s3[0], s3[1]):
+        for scales in (s1[0], s3[0]):
             nc.vector.memset(as_int32(scales), 0)
         nc.gpsimd.memset(x_scales[:], 0)
         make_identity(nc, ident[:])
@@ -61,7 +61,7 @@ def tile_moe_tk_glu_relu_kernel(
         x_f32 = []
         t0 = 0
         for tokens, by_vector in X_TILES:
-            chunk = held.tile([P, PACK, tokens], F32, name=f"x_f32_{t0}")
+            chunk = held.tile([P, PACK, tokens], F32, name=f"x_f32_{t0}", tag=f"x_f32_{t0}", align_bytes=64)
             nc.sync.dma_start(chunk[:], x_rows[:, :, t0 : t0 + tokens])
             x_f32.append((t0, tokens, by_vector, chunk))
             t0 = t0 + tokens
@@ -91,15 +91,19 @@ def tile_moe_tk_glu_relu_kernel(
         def w2(*experts):
             load_words("w2", w2_words, w2_sb, N, experts)
 
-        load_scales(s1[0], w1_scales, *RANGES[0])
+        s3.append(held.tile([P, E - RANGES[1][0], H], U8, name="s3_1", align_bytes=64))
+        nc.vector.memset(as_int32(s3[1]), 0)
+        load_scales(s3[1], w3_scales, *RANGES[1], nc.gpsimd)
+
+        load_scales(s1[0], w1_scales, 0, E)
         w1(0, 1)
         w1(2, 3, 4, 5)
-        load_scales(s1[1], w1_scales, *RANGES[1])
-        w1(6, 7, 8)
         load_scales(s3[0], w3_scales, *RANGES[0])
-        w3(0, 1, 2)
-        w3(3, 4, 5)
-        load_scales(s3[1], w3_scales, *RANGES[1])
+        w3(0, 1)
+        w1(6, 7)
+        w3(2, 3)
+        w3(4, 5)
+        w1(8)
         w3(6, 7)
         w1(9, 10, 11)
         w3(8, 9)
@@ -147,15 +151,15 @@ def tile_moe_tk_glu_relu_kernel(
         def by_pairs(acc):
             return acc.rearrange("c (p u v) -> c u p v", u=2, v=2)
 
-        def first_layer(e, name, bank, w, s):
+        def first_layer(e, name, bank, w, s, ranges):
             acc = psum.tile([C, H], F32, name=f"{name}_{e}", offset=bank * BANK)
-            part = [e0 <= e < e1 for e0, e1 in RANGES].index(True)
+            part = [e0 <= e < e1 for e0, e1 in ranges].index(True)
             nc.tensor.matmul_mx(
                 out=acc[:],
                 lhsT=codes_of[e].bitcast(FP8X4),
                 lhsT_scale=scales_of[e],
                 rhs=w[e].bitcast(FP4X4),
-                rhs_scale=s[part][:, e - RANGES[part][0], :],
+                rhs_scale=s[part][:, e - ranges[part][0], :],
                 start=True,
                 stop=True,
             )
@@ -166,14 +170,14 @@ def tile_moe_tk_glu_relu_kernel(
 
         def A(*experts):
             for e in experts:
-                a = first_layer(e, "a", A_BANK[e], w1_sb, s1)
+                a = first_layer(e, "a", A_BANK[e], w1_sb, s1, [(0, E)])
                 relu_a = held.tile([C, 2, P, 2], F32, name=f"relu_a_{e}", tag=f"relu_a_{e}", align_bytes=64)
                 nc.scalar.activation(relu_a[:], by_pairs(a[:]), RELU)
                 relu_of[e] = relu_a
 
         def B(*experts):
             for e in experts:
-                b_of[e] = first_layer(e, "b", B_BANK[e], w3_sb, s3)
+                b_of[e] = first_layer(e, "b", B_BANK[e], w3_sb, s3, RANGES)
 
         def M(*experts):
             for e in experts:
@@ -237,31 +241,33 @@ def tile_moe_tk_glu_relu_kernel(
         s2 = held.tile([P, E, N], U8, name="s2", tag="x_words", align_bytes=64)
         nc.gpsimd.memset(as_int32(s2), 0)
         load_scales(s2, w2_scales, 0, E, nc.gpsimd)
-        A(0, 1, 2, 3, 4, 5, 6, 7, 8)
-        B(0, 1, 2, 3, 4, 5)
+        A(0, 1, 2, 3, 4, 5)
+        B(0, 1)
+        A(6, 7)
+        B(2, 3, 4, 5)
+        A(8)
         M(0, 1)
         turn(0)
+        B(6, 7)
         M(2, 3)
         turn(1)
-        B(6, 7)
         M(4, 5)
         Q(0)
         Q(1)
         A(9, 10, 11)
         B(8, 9)
-        B(10, 11)
         M(6)
-        turn(2)
+        B(10, 11)
         M(7)
+        turn(2)
         turn(3)
         M(8, 9)
         turn(4)
-        Q(2)
         M(10)
         turn(5)
         M(11)
         turn(6)
-        for g in range(3, 7):
+        for g in range(2, 7):
             Q(g)
         for j in range(4):
             Y(j)

@@ -24,15 +24,12 @@ ADD = mybir.AluOpType.add
 RELU = mybir.ActivationFunctionType.Relu
 
 BANK = 2048
-GATHERS = [(0,), (1, 2), (3, 4, 5), (6, 7, 8), (9, 10), (11,)]
-GROUPS = [(0, 1), (2, 3), (4, 5), (6, 7), (8, 9), (10,), (11,)]
-RANGES = [(0, 6), (6, 12)]
-A_BANK = [0, 1, 2, 3, 0, 1, 2, 3, 2, 7, 0, 1]
-B_BANK = [4, 5, 6, 7, 0, 1, 5, 4, 3, 6, 5, 2]
-T_BANK = [3, 6, 4, 7, 0, 1, 4]
-Y_TILES = [((0, 1, 2, 3), 3, False), ((4, 5, 6, 7), 6, False), ((8, 9), 5, True), ((10, 11), 7, True)]
-X_TILES = [(256, 160), (256, 160)]
-CUT = 384
+X_TOKENS = 256
+X_VECTOR = 160
+EARLY = 6
+GATHERED = 3
+HALF = 256
+TURNED = [(0, 1), (2, 3), (4, 5), (6, 7), (8, 9), (10,), (11,)]
 
 
 def tile_moe_tk_glu_relu_kernel(
@@ -43,8 +40,8 @@ def tile_moe_tk_glu_relu_kernel(
         held = ctx.enter_context(tc.tile_pool(name="held", bufs=1))
         psum = ctx.enter_context(tc.psum_pool(name="psum", bufs=1))
 
-        s1 = [held.tile([P, E, H], U8, name="s1", align_bytes=64)]
-        s3 = [held.tile([P, RANGES[0][1], H], U8, name="s3_0", align_bytes=64)]
+        s1 = held.tile([P, E, H], U8, name="s1", align_bytes=64)
+        s3_early = held.tile([P, EARLY, H], U8, name="s3_early", align_bytes=64)
         x_words = held.tile([P, T], U32, name="x_words", tag="x_words", align_bytes=64)
         x_scales = held.tile([P, T], U8, name="x_scales", align_bytes=64)
         ident = held.tile([P, P], F32, name="ident")
@@ -52,23 +49,20 @@ def tile_moe_tk_glu_relu_kernel(
         def as_int32(scales):
             return scales[:].rearrange("p e i -> p (e i)").bitcast(I32)
 
-        for scales in (s1[0], s3[0]):
+        for scales in (s1, s3_early):
             nc.vector.memset(as_int32(scales), 0)
         nc.gpsimd.memset(x_scales[:], 0)
         make_identity(nc, ident[:])
 
         x_rows = xT.rearrange("(p j) t -> p j t", j=PACK)
-        x_f32 = []
-        t0 = 0
-        for tokens, by_vector in X_TILES:
-            chunk = held.tile([P, PACK, tokens], F32, name=f"x_f32_{t0}", tag=f"x_f32_{t0}", align_bytes=64)
-            nc.sync.dma_start(chunk[:], x_rows[:, :, t0 : t0 + tokens])
-            x_f32.append((t0, tokens, by_vector, chunk))
-            t0 = t0 + tokens
+        x_f32 = {}
+        for t0 in range(0, T, X_TOKENS):
+            x_f32[t0] = held.tile([P, PACK, X_TOKENS], F32, name=f"x_f32_{t0}", align_bytes=64)
+            nc.sync.dma_start(x_f32[t0][:], x_rows[:, :, t0 : t0 + X_TOKENS])
         offs_sb = held.tile([P, S // 16], U16, name="offs_sb")
         nc.sync.dma_start(offs_sb[:], offs)
 
-        def load_scales(tile, scales, e0, e1, queue=nc.sync):
+        def load_scales(queue, tile, scales, e0, e1):
             rows = scales[e0:e1, 0].rearrange("e (q r) i -> r q e i", r=4)
             for r in range(4):
                 queue.dma_start(tile[r:P:32, :, :].bitcast(I32), rows[r].bitcast(I32))
@@ -77,39 +71,39 @@ def tile_moe_tk_glu_relu_kernel(
 
         def load_words(name, words, by_expert, width, experts):
             e0, n = experts[0], len(experts)
-            w = held.tile([P, n, 2 * width], U8, name=f"{name}_{e0}", tag=f"{name}_{e0}", align_bytes=64)
+            w = held.tile([P, n, 2 * width], U8, name=f"{name}_{e0}", align_bytes=64)
             nc.sync.dma_start(w[:].bitcast(I32), words[e0 : e0 + n, 0].rearrange("e p b -> p e b").bitcast(I32))
             for k in range(n):
                 by_expert[e0 + k] = w[:, k, :]
 
-        def w1(*experts):
+        def load_w1(*experts):
             load_words("w1", w1_words, w1_sb, H, experts)
 
-        def w3(*experts):
+        def load_w3(*experts):
             load_words("w3", w3_words, w3_sb, H, experts)
 
-        def w2(*experts):
+        def load_w2(*experts):
             load_words("w2", w2_words, w2_sb, N, experts)
 
-        s3.append(held.tile([P, E - RANGES[1][0], H], U8, name="s3_1", align_bytes=64))
-        nc.vector.memset(as_int32(s3[1]), 0)
-        load_scales(s3[1], w3_scales, *RANGES[1], nc.gpsimd)
+        s3_late = held.tile([P, E - EARLY, H], U8, name="s3_late", align_bytes=64)
+        nc.vector.memset(as_int32(s3_late), 0)
+        load_scales(nc.gpsimd, s3_late, w3_scales, EARLY, E)
 
-        load_scales(s1[0], w1_scales, 0, E)
-        w1(0, 1)
-        w1(2, 3, 4, 5)
-        load_scales(s3[0], w3_scales, *RANGES[0])
-        w3(0, 1)
-        w1(6, 7)
-        w3(2, 3)
-        w3(4, 5)
-        w1(8)
-        w3(6, 7)
-        w1(9, 10, 11)
-        w3(8, 9)
-        w3(10, 11)
-        w2(0, 1, 2, 3, 4, 5, 6, 7)
-        w2(8, 9, 10, 11)
+        load_scales(nc.sync, s1, w1_scales, 0, E)
+        load_w1(0, 1)
+        load_w1(2, 3, 4, 5)
+        load_scales(nc.sync, s3_early, w3_scales, 0, EARLY)
+        load_w3(0, 1)
+        load_w1(6, 7)
+        load_w3(2, 3)
+        load_w3(4, 5)
+        load_w1(8)
+        load_w3(6, 7)
+        load_w1(9, 10, 11)
+        load_w3(8, 9)
+        load_w3(10, 11)
+        load_w2(0, 1, 2, 3, 4, 5, 6, 7)
+        load_w2(8, 9, 10, 11)
         pos_sb = []
         for r, pos in enumerate((pos1, pos2, pos3)):
             places = held.tile([P, T // 16], U16, name=f"pos_sb_{r}")
@@ -121,170 +115,167 @@ def tile_moe_tk_glu_relu_kernel(
             nc.sync.dma_start(weights[:], gate[r])
             gate_sb.append(weights)
 
-        x_bf16 = []
-        for t0, tokens, by_vector, chunk in x_f32:
-            rounded = held.tile([P, tokens, PACK], BF16, name=f"x_bf16_{t0}", align_bytes=64)
-            rows = chunk[:].rearrange("p j t -> p t j")
-            nc.vector.tensor_copy(rounded[:, :by_vector, :], rows[:, :by_vector, :])
-            nc.scalar.copy(rounded[:, by_vector:, :], rows[:, by_vector:, :])
-            x_bf16.append((t0, tokens, rounded))
-        for t0, tokens, rounded in x_bf16:
+        x_bf16 = {}
+        for t0, chunk in x_f32.items():
+            x_bf16[t0] = held.tile([P, X_TOKENS, PACK], BF16, name=f"x_bf16_{t0}", align_bytes=64)
+            by_token = chunk[:].rearrange("p j t -> p t j")
+            nc.vector.tensor_copy(x_bf16[t0][:, :X_VECTOR, :], by_token[:, :X_VECTOR, :])
+            nc.scalar.copy(x_bf16[t0][:, X_VECTOR:, :], by_token[:, X_VECTOR:, :])
+        for t0, rounded in x_bf16.items():
             nc.vector.quantize_mx(
-                out=x_words[:, t0 : t0 + tokens].bitcast(FP8X4),
-                scales=x_scales[:, t0 : t0 + tokens],
+                out=x_words[:, t0 : t0 + X_TOKENS].bitcast(FP8X4),
+                scales=x_scales[:, t0 : t0 + X_TOKENS],
                 in_=rounded[:].rearrange("p t j -> p (t j)"),
             )
 
-        codes_of, scales_of = {}, {}
+        relu_of, b_of, h_of, rows_of, h_mx = {}, {}, {}, {}, {}
+        y_all = held.tile([N, S], F32, name="y_all")
 
-        def gather(group):
-            e0, n = group[0], len(group)
-            listed = offs_sb[:, e0 * C // 16 : (e0 + n) * C // 16]
-            codes = held.tile([P, n * C], U32, name=f"codes_{e0}", align_bytes=64)
-            scales = held.tile([P, n * C], U8, name=f"scales_{e0}", align_bytes=64)
+        x_mx = {}
+        for e0 in range(0, E, GATHERED):
+            listed = offs_sb[:, e0 * C // 16 : (e0 + GATHERED) * C // 16]
+            codes = held.tile([P, GATHERED * C], U32, name=f"codes_{e0}", align_bytes=64)
+            scales = held.tile([P, GATHERED * C], U8, name=f"scales_{e0}", align_bytes=64)
             nc.vector.tensor_copy(codes[:], x_words[:].indirect(listed))
             nc.vector.tensor_copy(scales[:], x_scales[:].indirect(listed))
-            for k, e in enumerate(group):
-                codes_of[e] = codes[:, k * C : (k + 1) * C]
-                scales_of[e] = scales[:, k * C : (k + 1) * C]
+            for k in range(GATHERED):
+                x_mx[e0 + k] = (codes[:, k * C : (k + 1) * C], scales[:, k * C : (k + 1) * C])
+
+        s2 = held.tile([P, E, N], U8, name="s2", tag="x_words", align_bytes=64)
+        nc.gpsimd.memset(as_int32(s2), 0)
+        load_scales(nc.gpsimd, s2, w2_scales, 0, E)
 
         def by_pairs(acc):
             return acc.rearrange("c (p u v) -> c u p v", u=2, v=2)
 
-        def first_layer(e, name, bank, w, s, ranges):
+        def first_layer(name, e, bank, words, scales):
             acc = psum.tile([C, H], F32, name=f"{name}_{e}", offset=bank * BANK)
-            part = [e0 <= e < e1 for e0, e1 in ranges].index(True)
             nc.tensor.matmul_mx(
                 out=acc[:],
-                lhsT=codes_of[e].bitcast(FP8X4),
-                lhsT_scale=scales_of[e],
-                rhs=w[e].bitcast(FP4X4),
-                rhs_scale=s[part][:, e - ranges[part][0], :],
+                lhsT=x_mx[e][0].bitcast(FP8X4),
+                lhsT_scale=x_mx[e][1],
+                rhs=words.bitcast(FP4X4),
+                rhs_scale=scales,
                 start=True,
                 stop=True,
             )
             return acc
 
-        relu_of, b_of, h_of, rows_of, y_banks = {}, {}, {}, {}, {}
-        y_all = held.tile([N, S], F32, name="y_all")
+        def relu_a(experts, banks):
+            for e, bank in zip(experts, banks):
+                a = first_layer("a", e, bank, w1_sb[e], s1[:, e, :])
+                relu_of[e] = held.tile([C, 2, P, 2], F32, name=f"relu_a_{e}", align_bytes=64)
+                nc.scalar.activation(relu_of[e][:], by_pairs(a[:]), RELU)
 
-        def A(*experts):
+        def make_b(experts, banks):
+            for e, bank in zip(experts, banks):
+                scales = s3_early[:, e, :] if e < EARLY else s3_late[:, e - EARLY, :]
+                b_of[e] = first_layer("b", e, bank, w3_sb[e], scales)
+
+        def product(*experts):
             for e in experts:
-                a = first_layer(e, "a", A_BANK[e], w1_sb, s1, [(0, E)])
-                relu_a = held.tile([C, 2, P, 2], F32, name=f"relu_a_{e}", tag=f"relu_a_{e}", align_bytes=64)
-                nc.scalar.activation(relu_a[:], by_pairs(a[:]), RELU)
-                relu_of[e] = relu_a
+                h_of[e] = held.tile([C, 2, P, 2], BF16, name=f"h_{e}")
+                nc.vector.tensor_tensor(h_of[e][:], by_pairs(b_of[e][:]), relu_of[e][:], MULT)
 
-        def B(*experts):
-            for e in experts:
-                b_of[e] = first_layer(e, "b", B_BANK[e], w3_sb, s3, RANGES)
-
-        def M(*experts):
-            for e in experts:
-                h = held.tile([C, 2, P, 2], BF16, name=f"h_{e}")
-                nc.vector.tensor_tensor(h[:], by_pairs(b_of[e][:]), relu_of[e][:], MULT)
-                h_of[e] = h
-
-        def G(*experts):
-            for e in experts:
-                h = held.tile([C, 2, P, 2], BF16, name=f"h_{e}")
-                b_sb = held.tile([C, 2, P, 2], F32, name=f"b_sb_{e}")
-                nc.scalar.copy(b_sb[:], by_pairs(b_of[e][:]))
-                nc.gpsimd.tensor_tensor(h[:], b_sb[:], relu_of[e][:], MULT)
-                h_of[e] = h
-
-        def turn(g, empty=nc.scalar.copy):
-            group = GROUPS[g]
-            n = len(group)
-            turned = psum.tile([P, n, 2, C], F32, name=f"turned_{g}", offset=T_BANK[g] * BANK)
+        def turn(g, bank):
+            group = TURNED[g]
+            turned = psum.tile([P, len(group), 2, C], F32, name=f"turned_{g}", offset=bank * BANK)
             for k, e in reversed(list(enumerate(group))):
                 words = h_of[e][:].rearrange("c u p v -> c (u p v)").bitcast(F32)
                 for u in range(2):
                     nc.tensor.transpose(turned[:, k, u, :], words[:, u * P : (u + 1) * P], ident[:])
-            h_rows = held.tile([P, n, C, PACK], BF16, name=f"h_rows_{g}", align_bytes=64)
-            empty(h_rows[:].bitcast(F32), turned[:].rearrange("p k u c -> p k c u"))
-            rows_of[g] = h_rows
+            rows_of[g] = held.tile([P, len(group), C, PACK], BF16, name=f"h_rows_{g}", align_bytes=64)
+            nc.scalar.copy(rows_of[g][:].bitcast(F32), turned[:].rearrange("p k u c -> p k c u"))
 
-        mx_of = {}
-
-        def Q(g, tag=None):
-            group = GROUPS[g]
-            n = len(group)
-            h_codes = held.tile([P, n * C], U32, name=f"h_codes_{g}", tag=tag or f"h_codes_{g}", align_bytes=64)
-            h_scales = held.tile([P, n * C], U8, name=f"h_scales_{g}", align_bytes=64)
+        def quantise_h(g):
+            group = TURNED[g]
+            h_codes = held.tile([P, len(group) * C], U32, name=f"h_codes_{g}", align_bytes=64)
+            h_scales = held.tile([P, len(group) * C], U8, name=f"h_scales_{g}", align_bytes=64)
             nc.vector.quantize_mx(
                 out=h_codes[:].bitcast(FP8X4),
                 scales=h_scales[:],
                 in_=rows_of[g][:].rearrange("p k c j -> p (k c j)"),
             )
             for k, e in enumerate(group):
-                mx_of[e] = (h_codes[:, k * C : (k + 1) * C], h_scales[:, k * C : (k + 1) * C])
+                h_mx[e] = (h_codes[:, k * C : (k + 1) * C], h_scales[:, k * C : (k + 1) * C])
 
-        def Y(j):
-            sharing, bank, by_vector = Y_TILES[j]
-            y = psum.tile([N, len(sharing) * C], F32, name=f"y_{j}", offset=bank * BANK)
-            for k, e in enumerate(sharing):
+        def second_layer(experts, bank, empty):
+            y = psum.tile([N, len(experts) * C], F32, name=f"y_{experts[0]}", offset=bank * BANK)
+            for k, e in enumerate(experts):
                 nc.tensor.matmul_mx(
                     out=y[:, k * C : (k + 1) * C],
                     lhsT=w2_sb[e].bitcast(FP4X4),
                     lhsT_scale=s2[:, e, :],
-                    rhs=mx_of[e][0].bitcast(FP8X4),
-                    rhs_scale=mx_of[e][1],
+                    rhs=h_mx[e][0].bitcast(FP8X4),
+                    rhs_scale=h_mx[e][1],
                     start=True,
                     stop=True,
                 )
-            empty = nc.vector.tensor_copy if by_vector else nc.scalar.copy
-            empty(y_all[:, sharing[0] * C : (sharing[-1] + 1) * C], y[:])
+            empty(y_all[:, experts[0] * C : (experts[-1] + 1) * C], y[:])
 
-        for group in GATHERS:
-            gather(group)
-        s2 = held.tile([P, E, N], U8, name="s2", tag="x_words", align_bytes=64)
-        nc.gpsimd.memset(as_int32(s2), 0)
-        load_scales(s2, w2_scales, 0, E, nc.gpsimd)
-        A(0, 1, 2, 3, 4, 5)
-        B(0, 1)
-        A(6, 7)
-        B(2, 3, 4, 5)
-        A(8)
-        M(0, 1)
-        turn(0)
-        B(6, 7)
-        M(2, 3)
-        turn(1)
-        M(4, 5)
-        Q(0)
-        Q(1)
-        A(9, 10, 11)
-        B(8, 9)
-        M(6)
-        B(10, 11)
-        M(7)
-        turn(2)
-        turn(3)
-        M(8, 9)
-        turn(4)
-        M(10)
-        turn(5)
-        M(11)
-        turn(6)
-        for g in range(2, 7):
-            Q(g)
-        for j in range(4):
-            Y(j)
-
-        parts = [held.tile([N, T], F32, name=f"part_{r}") for r in range(TOP)]
-        two = held.tile([N, T], F32, name="two")
-        total = held.tile([N, T], F32, name="total")
+        relu_a(range(6), banks=(0, 1, 2, 3, 0, 1))
+        make_b((0, 1), banks=(4, 5))
+        relu_a((6, 7), banks=(2, 3))
+        make_b((2, 3, 4, 5), banks=(6, 7, 0, 1))
+        relu_a((8,), banks=(2,))
+        product(0, 1)
+        turn(0, bank=3)
+        make_b((6, 7), banks=(5, 4))
+        product(2, 3)
+        turn(1, bank=6)
+        product(4, 5)
+        quantise_h(0)
+        quantise_h(1)
+        relu_a((9, 10, 11), banks=(7, 0, 1))
+        make_b((8, 9), banks=(3, 6))
+        product(6)
+        make_b((10, 11), banks=(5, 2))
+        product(7)
+        turn(2, bank=4)
+        turn(3, bank=7)
+        product(8, 9)
+        turn(4, bank=0)
+        product(10)
+        turn(5, bank=1)
+        product(11)
+        turn(6, bank=4)
+        for g in range(2, len(TURNED)):
+            quantise_h(g)
+        second_layer((0, 1, 2, 3), 3, nc.scalar.copy)
+        second_layer((4, 5, 6, 7), 6, nc.scalar.copy)
+        second_layer((8, 9), 5, nc.vector.tensor_copy)
+        second_layer((10, 11), 7, nc.vector.tensor_copy)
 
         def fetch(r, t0, t1):
+            part = held.tile([N, t1 - t0], F32, name=f"part_{r}_{t0}")
             listed = pos_sb[r][:, t0 // 16 : t1 // 16]
-            nc.vector.tensor_tensor(parts[r][:, t0:t1], y_all[:].indirect(listed), gate_sb[r][:, t0:t1], MULT)
+            nc.vector.tensor_tensor(part[:], y_all[:].indirect(listed), gate_sb[r][:, t0:t1], MULT)
+            return part
 
-        fetch(0, 0, T)
-        fetch(1, 0, T)
-        fetch(2, 0, CUT)
-        nc.vector.tensor_tensor(two[:], parts[0][:], parts[1][:], ADD)
-        fetch(2, CUT, T)
-        for t0, t1 in ((0, CUT), (CUT, T)):
-            nc.vector.tensor_tensor(total[:, t0:t1], two[:, t0:t1], parts[2][:, t0:t1], ADD)
-            nc.sync.dma_start(out[:, t0:t1], total[:, t0:t1])
+        first = [fetch(r, 0, HALF) for r in range(TOP)]
+        blocks = HALF // P
+        sums = [psum.tile([P, N], F32, name=f"sum_{j}", offset=j * BANK) for j in range(blocks)]
+        for r in range(TOP):
+            for j in range(blocks):
+                nc.tensor.matmul(
+                    sums[j][:],
+                    first[r][:, j * P : (j + 1) * P],
+                    ident[:],
+                    start=r == 0,
+                    stop=r == TOP - 1,
+                    is_transpose=True,
+                )
+        back = psum.tile([N, HALF], F32, name="back", offset=blocks * BANK)
+        for j in range(blocks):
+            summed = held.tile([P, N], F32, name=f"sum_sb_{j}")
+            nc.scalar.copy(summed[:], sums[j][:])
+            nc.tensor.transpose(back[:, j * P : (j + 1) * P], summed[:], ident[:])
+        first_total = held.tile([N, HALF], F32, name="first_total")
+        nc.scalar.copy(first_total[:], back[:])
+        rest = [fetch(r, HALF, T) for r in range(TOP)]
+        two = held.tile([N, T - HALF], F32, name="two")
+        rest_total = held.tile([N, T - HALF], F32, name="rest_total")
+        nc.vector.tensor_tensor(two[:], rest[0][:], rest[1][:], ADD)
+        nc.vector.tensor_tensor(rest_total[:], two[:], rest[2][:], ADD)
+        nc.scalar.dma_start(out[:, :HALF], first_total[:])
+        nc.sync.dma_start(out[:, HALF:], rest_total[:])

@@ -22,12 +22,14 @@ FP4X4 = mybir.dt.float4_e2m1fn_x4
 MULT = mybir.AluOpType.mult
 ADD = mybir.AluOpType.add
 RELU = mybir.ActivationFunctionType.Relu
+COPY = mybir.ActivationFunctionType.Copy
 
 BANK = 2048
 X_TOKENS = 256
 X_VECTOR = 160
-EARLY = 6
-GATHERED = 3
+GATHERED = [(0,), (1, 2), (3, 4, 5), (6, 7, 8), (9, 10, 11)]
+S1_EARLY = 3
+ON_GPSIMD = 2
 HALF = 256
 TURNED = [(0, 1), (2, 3), (4, 5), (6, 7), (8, 9), (10,), (11,)]
 
@@ -40,19 +42,37 @@ def tile_moe_tk_glu_relu_kernel(
         held = ctx.enter_context(tc.tile_pool(name="held", bufs=1))
         psum = ctx.enter_context(tc.psum_pool(name="psum", bufs=1))
 
-        s1 = held.tile([P, E, H], U8, name="s1", align_bytes=64)
-        s3_early = held.tile([P, EARLY, H], U8, name="s3_early", align_bytes=64)
-        x_words = held.tile([P, T], U32, name="x_words", tag="x_words", align_bytes=64)
+        s1_of, s3_of, s2_of = {}, {}, {}
+
+        def scale_tile(name, by_expert, width, e0, e1):
+            tile = held.tile([P, e1 - e0, width], U8, name=f"{name}_{e0}", align_bytes=64)
+            for e in range(e0, e1):
+                by_expert[e] = tile[:, e - e0, :]
+            return tile
+
+        s1_early, s1_late = scale_tile("s1", s1_of, H, 0, S1_EARLY), scale_tile("s1", s1_of, H, S1_EARLY, E)
+        s3_early, s3_late = scale_tile("s3", s3_of, H, 0, ON_GPSIMD), scale_tile("s3", s3_of, H, ON_GPSIMD, E)
+        s2 = scale_tile("s2", s2_of, N, 0, E)
+        x_words = held.tile([P, T], U32, name="x_words", align_bytes=64)
         x_scales = held.tile([P, T], U8, name="x_scales", align_bytes=64)
         ident = held.tile([P, P], F32, name="ident")
 
         def as_int32(scales):
             return scales[:].rearrange("p e i -> p (e i)").bitcast(I32)
 
-        for scales in (s1, s3_early):
-            nc.vector.memset(as_int32(scales), 0)
-        nc.gpsimd.memset(x_scales[:], 0)
+        def load_scales(queue, tile, scales, e0, e1):
+            rows = scales[e0:e1, 0].rearrange("e (q r) i -> r q e i", r=4)
+            for r in range(4):
+                queue.dma_start(tile[r:P:32, :, :].bitcast(I32), rows[r].bitcast(I32))
+
         make_identity(nc, ident[:])
+        nc.vector.memset(as_int32(s3_late), 0)
+        load_scales(nc.gpsimd, s3_late, w3_scales, ON_GPSIMD, E)
+        nc.gpsimd.memset(as_int32(s2), 0)
+        for words in (as_int32(s1_early), as_int32(s3_early), x_scales[:].bitcast(I32), as_int32(s1_late)):
+            cut = words.shape[1] // 2 - 1
+            nc.vector.memset(words[:, :cut], 0)
+            nc.vector.memset(words[:, cut:], 0)
 
         x_rows = xT.rearrange("(p j) t -> p j t", j=PACK)
         x_f32 = {}
@@ -61,11 +81,6 @@ def tile_moe_tk_glu_relu_kernel(
             nc.sync.dma_start(x_f32[t0][:], x_rows[:, :, t0 : t0 + X_TOKENS])
         offs_sb = held.tile([P, S // 16], U16, name="offs_sb")
         nc.sync.dma_start(offs_sb[:], offs)
-
-        def load_scales(queue, tile, scales, e0, e1):
-            rows = scales[e0:e1, 0].rearrange("e (q r) i -> r q e i", r=4)
-            for r in range(4):
-                queue.dma_start(tile[r:P:32, :, :].bitcast(I32), rows[r].bitcast(I32))
 
         w1_sb, w3_sb, w2_sb = {}, {}, {}
 
@@ -85,35 +100,32 @@ def tile_moe_tk_glu_relu_kernel(
         def load_w2(*experts):
             load_words("w2", w2_words, w2_sb, N, experts)
 
-        s3_late = held.tile([P, E - EARLY, H], U8, name="s3_late", align_bytes=64)
-        nc.vector.memset(as_int32(s3_late), 0)
-        load_scales(nc.gpsimd, s3_late, w3_scales, EARLY, E)
-
-        load_scales(nc.sync, s1, w1_scales, 0, E)
-        load_w1(0, 1)
-        load_w1(2, 3, 4, 5)
-        load_scales(nc.sync, s3_early, w3_scales, 0, EARLY)
+        load_scales(nc.sync, s1_early, w1_scales, 0, S1_EARLY)
+        load_w1(0)
+        load_scales(nc.sync, s3_early, w3_scales, 0, ON_GPSIMD)
         load_w3(0, 1)
-        load_w1(6, 7)
+        load_w1(1, 2)
+        load_scales(nc.sync, s1_late, w1_scales, S1_EARLY, E)
+        load_w1(3, 4, 5)
+        load_w1(6, 7, 8)
+        load_scales(nc.sync, s2, w2_scales, 0, E)
         load_w3(2, 3)
         load_w3(4, 5)
-        load_w1(8)
-        load_w3(6, 7)
         load_w1(9, 10, 11)
+        load_w3(6, 7)
         load_w3(8, 9)
         load_w3(10, 11)
-        load_w2(0, 1, 2, 3, 4, 5, 6, 7)
-        load_w2(8, 9, 10, 11)
+        load_w2(0, 1, 2, 3, 4, 5)
+        load_w2(6, 7, 8, 9, 10, 11)
         pos_sb = []
         for r, pos in enumerate((pos1, pos2, pos3)):
             places = held.tile([P, T // 16], U16, name=f"pos_sb_{r}")
             nc.sync.dma_start(places[:], pos)
             pos_sb.append(places)
-        gate_sb = []
-        for r in range(TOP):
-            weights = held.tile([N, T], F32, name=f"gate_sb_{r}")
-            nc.sync.dma_start(weights[:], gate[r])
-            gate_sb.append(weights)
+        gate_sb = {}
+        for t0 in range(0, T, HALF):
+            gate_sb[t0] = held.tile([N, TOP, HALF], F32, name=f"gate_sb_{t0}")
+            nc.sync.dma_start(gate_sb[t0][:], gate[:, :, t0 : t0 + HALF].rearrange("r n t -> n r t"))
 
         x_bf16 = {}
         for t0, chunk in x_f32.items():
@@ -132,18 +144,15 @@ def tile_moe_tk_glu_relu_kernel(
         y_all = held.tile([N, S], F32, name="y_all")
 
         x_mx = {}
-        for e0 in range(0, E, GATHERED):
-            listed = offs_sb[:, e0 * C // 16 : (e0 + GATHERED) * C // 16]
-            codes = held.tile([P, GATHERED * C], U32, name=f"codes_{e0}", align_bytes=64)
-            scales = held.tile([P, GATHERED * C], U8, name=f"scales_{e0}", align_bytes=64)
-            nc.vector.tensor_copy(codes[:], x_words[:].indirect(listed))
-            nc.vector.tensor_copy(scales[:], x_scales[:].indirect(listed))
-            for k in range(GATHERED):
-                x_mx[e0 + k] = (codes[:, k * C : (k + 1) * C], scales[:, k * C : (k + 1) * C])
-
-        s2 = held.tile([P, E, N], U8, name="s2", tag="x_words", align_bytes=64)
-        nc.gpsimd.memset(as_int32(s2), 0)
-        load_scales(nc.gpsimd, s2, w2_scales, 0, E)
+        for group in GATHERED:
+            e0, n = group[0], len(group)
+            slots = offs_sb[:, e0 * C // 16 : (e0 + n) * C // 16]
+            codes = held.tile([P, n * C], U32, name=f"codes_{e0}", align_bytes=64)
+            scales = held.tile([P, n * C], U8, name=f"scales_{e0}", align_bytes=64)
+            nc.vector.tensor_copy(codes[:], x_words[:].indirect(slots))
+            nc.vector.tensor_copy(scales[:], x_scales[:].indirect(slots))
+            for k, e in enumerate(group):
+                x_mx[e] = (codes[:, k * C : (k + 1) * C], scales[:, k * C : (k + 1) * C])
 
         def by_pairs(acc):
             return acc.rearrange("c (p u v) -> c u p v", u=2, v=2)
@@ -163,19 +172,25 @@ def tile_moe_tk_glu_relu_kernel(
 
         def relu_a(experts, banks):
             for e, bank in zip(experts, banks):
-                a = first_layer("a", e, bank, w1_sb[e], s1[:, e, :])
-                relu_of[e] = held.tile([C, 2, P, 2], F32, name=f"relu_a_{e}", align_bytes=64)
+                a = first_layer("a", e, bank, w1_sb[e], s1_of[e])
+                relu_of[e] = held.tile([C, 2, P, 2], F32, name=f"relu_a_{e}", tag=f"relu_a_{e}", align_bytes=64)
                 nc.scalar.activation(relu_of[e][:], by_pairs(a[:]), RELU)
 
         def make_b(experts, banks):
             for e, bank in zip(experts, banks):
-                scales = s3_early[:, e, :] if e < EARLY else s3_late[:, e - EARLY, :]
-                b_of[e] = first_layer("b", e, bank, w3_sb[e], scales)
+                b_of[e] = first_layer("b", e, bank, w3_sb[e], s3_of[e])
 
         def product(*experts):
             for e in experts:
                 h_of[e] = held.tile([C, 2, P, 2], BF16, name=f"h_{e}")
                 nc.vector.tensor_tensor(h_of[e][:], by_pairs(b_of[e][:]), relu_of[e][:], MULT)
+
+        def product_on_gpsimd(e, bank):
+            make_b((e,), (bank,))
+            b_sb = held.tile([C, 2, P, 2], F32, name=f"b_sb_{e}")
+            nc.scalar.copy(b_sb[:], by_pairs(b_of[e][:]))
+            h_of[e] = held.tile([C, 2, P, 2], BF16, name=f"h_{e}")
+            nc.gpsimd.tensor_tensor(h_of[e][:], b_sb[:], relu_of[e][:], MULT)
 
         def turn(g, bank):
             group = TURNED[g]
@@ -187,9 +202,10 @@ def tile_moe_tk_glu_relu_kernel(
             rows_of[g] = held.tile([P, len(group), C, PACK], BF16, name=f"h_rows_{g}", align_bytes=64)
             nc.scalar.copy(rows_of[g][:].bitcast(F32), turned[:].rearrange("p k u c -> p k c u"))
 
-        def quantise_h(g):
+        def quantise_h(g, after=None):
             group = TURNED[g]
-            h_codes = held.tile([P, len(group) * C], U32, name=f"h_codes_{g}", align_bytes=64)
+            tag = f"h_codes_{g}" if after is None else f"relu_a_{after}"
+            h_codes = held.tile([P, len(group) * C], U32, name=f"h_codes_{g}", tag=tag, align_bytes=64)
             h_scales = held.tile([P, len(group) * C], U8, name=f"h_scales_{g}", align_bytes=64)
             nc.vector.quantize_mx(
                 out=h_codes[:].bitcast(FP8X4),
@@ -205,7 +221,7 @@ def tile_moe_tk_glu_relu_kernel(
                 nc.tensor.matmul_mx(
                     out=y[:, k * C : (k + 1) * C],
                     lhsT=w2_sb[e].bitcast(FP4X4),
-                    lhsT_scale=s2[:, e, :],
+                    lhsT_scale=s2_of[e],
                     rhs=h_mx[e][0].bitcast(FP8X4),
                     rhs_scale=h_mx[e][1],
                     start=True,
@@ -213,69 +229,77 @@ def tile_moe_tk_glu_relu_kernel(
                 )
             empty(y_all[:, experts[0] * C : (experts[-1] + 1) * C], y[:])
 
-        relu_a(range(6), banks=(0, 1, 2, 3, 0, 1))
-        make_b((0, 1), banks=(4, 5))
-        relu_a((6, 7), banks=(2, 3))
-        make_b((2, 3, 4, 5), banks=(6, 7, 0, 1))
-        relu_a((8,), banks=(2,))
-        product(0, 1)
-        turn(0, bank=3)
-        make_b((6, 7), banks=(5, 4))
-        product(2, 3)
-        turn(1, bank=6)
+        for e, bank in zip(range(ON_GPSIMD), (7, 3)):
+            relu_a((e,), banks=(e,))
+            product_on_gpsimd(e, bank)
+        relu_a((2,), banks=(2,))
+        relu_a(range(3, 9), banks=(0, 1, 2, 0, 1, 7))
+        make_b((2, 3, 4, 5), banks=(3, 4, 5, 6))
+        relu_a((9, 10, 11), banks=(2, 0, 1))
+        make_b((6,), banks=(7,))
+        product(2)
+        make_b((7,), banks=(3,))
+        product(3)
+        turn(0, bank=2)
+        turn(1, bank=0)
+        make_b((8,), banks=(4,))
         product(4, 5)
+        turn(2, bank=1)
+        make_b((9, 10), banks=(5, 6))
+        product(6, 7)
+        turn(3, bank=2)
+        make_b((11,), banks=(7,))
         quantise_h(0)
         quantise_h(1)
-        relu_a((9, 10, 11), banks=(7, 0, 1))
-        make_b((8, 9), banks=(3, 6))
-        product(6)
-        make_b((10, 11), banks=(5, 2))
-        product(7)
-        turn(2, bank=4)
-        turn(3, bank=7)
+        second_layer((0, 1, 2, 3), 3, nc.scalar.copy)
         product(8, 9)
+        quantise_h(2)
         turn(4, bank=0)
         product(10)
         turn(5, bank=1)
         product(11)
         turn(6, bank=4)
-        for g in range(2, len(TURNED)):
+        quantise_h(3, after=10)
+        for g in range(4, len(TURNED)):
             quantise_h(g)
-        second_layer((0, 1, 2, 3), 3, nc.scalar.copy)
-        second_layer((4, 5, 6, 7), 6, nc.scalar.copy)
-        second_layer((8, 9), 5, nc.vector.tensor_copy)
-        second_layer((10, 11), 7, nc.vector.tensor_copy)
+        second_layer((4, 5, 6, 7), 2, nc.scalar.copy)
+        second_layer((8, 9), 5, nc.scalar.copy)
+        second_layer((10, 11), 6, nc.vector.tensor_copy)
 
-        def fetch(r, t0, t1):
-            part = held.tile([N, t1 - t0], F32, name=f"part_{r}_{t0}")
-            listed = pos_sb[r][:, t0 // 16 : t1 // 16]
-            nc.vector.tensor_tensor(part[:], y_all[:].indirect(listed), gate_sb[r][:, t0:t1], MULT)
-            return part
+        def listed(r, t0):
+            return y_all[:].indirect(pos_sb[r][:, t0 // 16 : (t0 + HALF) // 16])
 
-        first = [fetch(r, 0, HALF) for r in range(TOP)]
-        blocks = HALF // P
-        sums = [psum.tile([P, N], F32, name=f"sum_{j}", offset=j * BANK) for j in range(blocks)]
-        for r in range(TOP):
-            for j in range(blocks):
-                nc.tensor.matmul(
-                    sums[j][:],
-                    first[r][:, j * P : (j + 1) * P],
-                    ident[:],
-                    start=r == 0,
-                    stop=r == TOP - 1,
-                    is_transpose=True,
-                )
-        back = psum.tile([N, HALF], F32, name="back", offset=blocks * BANK)
-        for j in range(blocks):
-            summed = held.tile([P, N], F32, name=f"sum_sb_{j}")
-            nc.scalar.copy(summed[:], sums[j][:])
-            nc.tensor.transpose(back[:, j * P : (j + 1) * P], summed[:], ident[:])
-        first_total = held.tile([N, HALF], F32, name="first_total")
-        nc.scalar.copy(first_total[:], back[:])
-        rest = [fetch(r, HALF, T) for r in range(TOP)]
-        two = held.tile([N, T - HALF], F32, name="two")
-        rest_total = held.tile([N, T - HALF], F32, name="rest_total")
-        nc.vector.tensor_tensor(two[:], rest[0][:], rest[1][:], ADD)
-        nc.vector.tensor_tensor(rest_total[:], two[:], rest[2][:], ADD)
-        nc.scalar.dma_start(out[:, :HALF], first_total[:])
-        nc.sync.dma_start(out[:, HALF:], rest_total[:])
+        def part(name, r, t0):
+            return held.tile([N, HALF], F32, name=f"{name}_{r}_{t0}")
+
+        fetched, gated = {}, {}
+
+        def fetch(r, t0):
+            fetched[r, t0] = part("fetched", r, t0)
+            nc.scalar.activation(fetched[r, t0][:], listed(r, t0), COPY)
+
+        def fetch_gated(r, t0):
+            gated[r, t0] = part("gated", r, t0)
+            nc.vector.tensor_tensor(gated[r, t0][:], listed(r, t0), gate_sb[t0][:, r, :], MULT)
+
+        def apply_gate(r, t0):
+            gated[r, t0] = part("gated", r, t0)
+            nc.vector.tensor_tensor(gated[r, t0][:], fetched[r, t0][:], gate_sb[t0][:, r, :], MULT)
+
+        def add(name, t0, first, second):
+            total = part(name, 0, t0)
+            nc.vector.tensor_tensor(total[:], first[:], second[:], ADD)
+            return total
+
+        for r, t0 in ((1, 0), (2, 0), (1, HALF), (2, HALF)):
+            fetch(r, t0)
+        fetch_gated(0, 0)
+        fetch_gated(0, HALF)
+        apply_gate(1, 0)
+        apply_gate(2, 0)
+        two = add("two", 0, gated[0, 0], gated[1, 0])
+        apply_gate(1, HALF)
+        nc.sync.dma_start(out[:, :HALF], add("three", 0, two, gated[2, 0])[:])
+        two = add("two", HALF, gated[0, HALF], gated[1, HALF])
+        apply_gate(2, HALF)
+        nc.sync.dma_start(out[:, HALF:], add("three", HALF, two, gated[2, HALF])[:])

@@ -28,7 +28,7 @@ BANK = 2048
 X_TOKENS = 256
 X_VECTOR = 160
 GATHERED = [(0,), (1, 2), (3, 4, 5), (6, 7, 8), (9, 10, 11)]
-S1_EARLY = 3
+S1_CUTS = (0, 3, 6, E)
 ON_GPSIMD = 2
 HALF = 256
 TURNED = [(0, 1), (2, 3), (4, 5), (6, 7), (8, 9), (10,), (11,)]
@@ -50,7 +50,7 @@ def tile_moe_tk_glu_relu_kernel(
                 by_expert[e] = tile[:, e - e0, :]
             return tile
 
-        s1_early, s1_late = scale_tile("s1", s1_of, H, 0, S1_EARLY), scale_tile("s1", s1_of, H, S1_EARLY, E)
+        s1 = [scale_tile("s1", s1_of, H, e0, e1) for e0, e1 in zip(S1_CUTS, S1_CUTS[1:])]
         s3_early, s3_late = scale_tile("s3", s3_of, H, 0, ON_GPSIMD), scale_tile("s3", s3_of, H, ON_GPSIMD, E)
         s2 = scale_tile("s2", s2_of, N, 0, E)
         x_words = held.tile([P, T], U32, name="x_words", align_bytes=64)
@@ -69,7 +69,7 @@ def tile_moe_tk_glu_relu_kernel(
         nc.vector.memset(as_int32(s3_late), 0)
         load_scales(nc.gpsimd, s3_late, w3_scales, ON_GPSIMD, E)
         nc.gpsimd.memset(as_int32(s2), 0)
-        for words in (as_int32(s1_early), as_int32(s3_early), x_scales[:].bitcast(I32), as_int32(s1_late)):
+        for words in (as_int32(s1[0]), as_int32(s3_early), x_scales[:].bitcast(I32), as_int32(s1[1]), as_int32(s1[2])):
             cut = words.shape[1] // 2 - 1
             nc.vector.memset(words[:, :cut], 0)
             nc.vector.memset(words[:, cut:], 0)
@@ -100,28 +100,32 @@ def tile_moe_tk_glu_relu_kernel(
         def load_w2(*experts):
             load_words("w2", w2_words, w2_sb, N, experts)
 
-        load_scales(nc.sync, s1_early, w1_scales, 0, S1_EARLY)
+        def load_s1(k):
+            load_scales(nc.sync, s1[k], w1_scales, S1_CUTS[k], S1_CUTS[k + 1])
+
+        load_s1(0)
         load_w1(0)
         load_scales(nc.sync, s3_early, w3_scales, 0, ON_GPSIMD)
         load_w3(0, 1)
         load_w1(1, 2)
-        load_scales(nc.sync, s1_late, w1_scales, S1_EARLY, E)
+        load_s1(1)
         load_w1(3, 4, 5)
+        load_s1(2)
         load_w1(6, 7, 8)
-        load_scales(nc.sync, s2, w2_scales, 0, E)
+        pos_sb = []
+        for r, pos in enumerate((pos1, pos2, pos3)):
+            places = held.tile([P, T // 16], U16, name=f"pos_sb_{r}")
+            nc.sync.dma_start(places[:], pos)
+            pos_sb.append(places)
         load_w3(2, 3)
         load_w3(4, 5)
         load_w1(9, 10, 11)
         load_w3(6, 7)
         load_w3(8, 9)
         load_w3(10, 11)
+        load_scales(nc.sync, s2, w2_scales, 0, E)
         load_w2(0, 1, 2, 3, 4, 5)
         load_w2(6, 7, 8, 9, 10, 11)
-        pos_sb = []
-        for r, pos in enumerate((pos1, pos2, pos3)):
-            places = held.tile([P, T // 16], U16, name=f"pos_sb_{r}")
-            nc.sync.dma_start(places[:], pos)
-            pos_sb.append(places)
         gate_sb = {}
         for t0 in range(0, T, HALF):
             gate_sb[t0] = held.tile([N, TOP, HALF], F32, name=f"gate_sb_{t0}")
@@ -253,18 +257,18 @@ def tile_moe_tk_glu_relu_kernel(
         quantise_h(1)
         second_layer((0, 1, 2, 3), 3, nc.scalar.copy)
         product(8, 9)
-        quantise_h(2)
         turn(4, bank=0)
         product(10)
         turn(5, bank=1)
         product(11)
         turn(6, bank=4)
+        quantise_h(2, after=9)
         quantise_h(3, after=10)
         for g in range(4, len(TURNED)):
             quantise_h(g)
-        second_layer((4, 5, 6, 7), 2, nc.scalar.copy)
-        second_layer((8, 9), 5, nc.scalar.copy)
-        second_layer((10, 11), 6, nc.vector.tensor_copy)
+        second_layer((4, 5, 6, 7), 2, nc.vector.tensor_copy)
+        second_layer((8, 9, 10), 5, nc.scalar.copy)
+        second_layer((11,), 6, nc.vector.tensor_copy)
 
         def listed(r, t0):
             return y_all[:].indirect(pos_sb[r][:, t0 // 16 : (t0 + HALF) // 16])

@@ -28,7 +28,7 @@ BANK = 2048
 X_TOKENS = 256
 X_VECTOR = 160
 GATHERED = [(0,), (1, 2), (3, 4, 5), (6, 7, 8), (9, 10, 11)]
-S1_CUTS = (0, 3, 6, E)
+S1_CUTS = (0, 6, E)
 ON_GPSIMD = 2
 HALF = 256
 TURNED = [(0, 1), (2, 3), (4, 5), (6, 7), (8, 9), (10,), (11,)]
@@ -69,7 +69,7 @@ def tile_moe_tk_glu_relu_kernel(
         nc.vector.memset(as_int32(s3_late), 0)
         load_scales(nc.gpsimd, s3_late, w3_scales, ON_GPSIMD, E)
         nc.gpsimd.memset(as_int32(s2), 0)
-        for words in (as_int32(s1[0]), as_int32(s3_early), x_scales[:].bitcast(I32), as_int32(s1[1]), as_int32(s1[2])):
+        for words in (as_int32(s1[0]), as_int32(s3_early), x_scales[:].bitcast(I32), as_int32(s1[1])):
             cut = words.shape[1] // 2 - 1
             nc.vector.memset(words[:, :cut], 0)
             nc.vector.memset(words[:, cut:], 0)
@@ -108,9 +108,8 @@ def tile_moe_tk_glu_relu_kernel(
         load_scales(nc.sync, s3_early, w3_scales, 0, ON_GPSIMD)
         load_w3(0, 1)
         load_w1(1, 2)
-        load_s1(1)
         load_w1(3, 4, 5)
-        load_s1(2)
+        load_s1(1)
         load_w1(6, 7, 8)
         pos_sb = []
         for r, pos in enumerate((pos1, pos2, pos3)):
@@ -126,10 +125,11 @@ def tile_moe_tk_glu_relu_kernel(
         load_scales(nc.sync, s2, w2_scales, 0, E)
         load_w2(0, 1, 2, 3, 4, 5)
         load_w2(6, 7, 8, 9, 10, 11)
-        gate_sb = {}
-        for t0 in range(0, T, HALF):
-            gate_sb[t0] = held.tile([N, TOP, HALF], F32, name=f"gate_sb_{t0}")
-            nc.sync.dma_start(gate_sb[t0][:], gate[:, :, t0 : t0 + HALF].rearrange("r n t -> n r t"))
+        gate_sb = []
+        for r in range(TOP):
+            weights = held.tile([N, T], F32, name=f"gate_sb_{r}")
+            nc.sync.dma_start(weights[:], gate[r])
+            gate_sb.append(weights)
 
         x_bf16 = {}
         for t0, chunk in x_f32.items():
@@ -284,11 +284,11 @@ def tile_moe_tk_glu_relu_kernel(
 
         def fetch_gated(r, t0):
             gated[r, t0] = part("gated", r, t0)
-            nc.vector.tensor_tensor(gated[r, t0][:], listed(r, t0), gate_sb[t0][:, r, :], MULT)
+            nc.vector.tensor_tensor(gated[r, t0][:], listed(r, t0), gate_sb[r][:, t0 : t0 + HALF], MULT)
 
         def apply_gate(r, t0):
             gated[r, t0] = part("gated", r, t0)
-            nc.vector.tensor_tensor(gated[r, t0][:], fetched[r, t0][:], gate_sb[t0][:, r, :], MULT)
+            nc.vector.tensor_tensor(gated[r, t0][:], fetched[r, t0][:], gate_sb[r][:, t0 : t0 + HALF], MULT)
 
         def add(name, t0, first, second):
             total = part(name, 0, t0)

@@ -69,10 +69,10 @@ def tile_moe_tk_glu_relu_kernel(
         nc.vector.memset(as_int32(s3_late), 0)
         load_scales(nc.gpsimd, s3_late, w3_scales, ON_GPSIMD, E)
         nc.gpsimd.memset(as_int32(s2), 0)
-        for words in (as_int32(s1[0]), as_int32(s3_early), x_scales[:].bitcast(I32), as_int32(s1[1])):
-            cut = words.shape[1] // 2 - 1
-            nc.vector.memset(words[:, :cut], 0)
-            nc.vector.memset(words[:, cut:], 0)
+        for zeroed in (as_int32(s1[0]), as_int32(s3_early), x_scales[:].bitcast(I32), as_int32(s1[1])):
+            cut = zeroed.shape[1] // 2 - 1
+            nc.vector.memset(zeroed[:, :cut], 0)
+            nc.vector.memset(zeroed[:, cut:], 0)
 
         x_rows = xT.rearrange("(p j) t -> p j t", j=PACK)
         x_f32 = {}
@@ -111,14 +111,14 @@ def tile_moe_tk_glu_relu_kernel(
         load_w1(3, 4, 5)
         load_s1(1)
         load_w1(6, 7, 8)
+        load_w3(2, 3)
         pos_sb = []
         for r, pos in enumerate((pos1, pos2, pos3)):
             places = held.tile([P, T // 16], U16, name=f"pos_sb_{r}")
             nc.sync.dma_start(places[:], pos)
             pos_sb.append(places)
-        load_w3(2, 3)
-        load_w3(4, 5)
         load_w1(9, 10, 11)
+        load_w3(4, 5)
         load_w3(6, 7)
         load_w3(8, 9)
         load_w3(10, 11)
@@ -127,9 +127,8 @@ def tile_moe_tk_glu_relu_kernel(
         load_w2(6, 7, 8, 9, 10, 11)
         gate_sb = []
         for r in range(TOP):
-            weights = held.tile([N, T], F32, name=f"gate_sb_{r}")
-            nc.sync.dma_start(weights[:], gate[r])
-            gate_sb.append(weights)
+            gate_sb.append(held.tile([N, T], F32, name=f"gate_sb_{r}"))
+            nc.sync.dma_start(gate_sb[r][:], gate[r])
 
         x_bf16 = {}
         for t0, chunk in x_f32.items():
@@ -236,11 +235,10 @@ def tile_moe_tk_glu_relu_kernel(
         for e, bank in zip(range(ON_GPSIMD), (7, 3)):
             relu_a((e,), banks=(e,))
             product_on_gpsimd(e, bank)
-        relu_a((2,), banks=(2,))
-        relu_a(range(3, 9), banks=(0, 1, 2, 0, 1, 7))
-        make_b((2, 3, 4, 5), banks=(3, 4, 5, 6))
+        relu_a(range(2, 9), banks=(2, 0, 1, 2, 0, 1, 7))
+        make_b((2, 3), banks=(3, 4))
         relu_a((9, 10, 11), banks=(2, 0, 1))
-        make_b((6,), banks=(7,))
+        make_b((4, 5, 6), banks=(5, 6, 7))
         product(2)
         make_b((7,), banks=(3,))
         product(3)
@@ -270,40 +268,39 @@ def tile_moe_tk_glu_relu_kernel(
         second_layer((8, 9, 10), 5, nc.scalar.copy)
         second_layer((11,), 6, nc.vector.tensor_copy)
 
-        def listed(r, t0):
-            return y_all[:].indirect(pos_sb[r][:, t0 // 16 : (t0 + HALF) // 16])
+        first = held.tile([N, T], F32, name="first")
+        fetched, gated = {}, {}
 
         def part(name, r, t0):
             return held.tile([N, HALF], F32, name=f"{name}_{r}_{t0}")
 
-        fetched, gated = {}, {}
-
         def fetch(r, t0):
             fetched[r, t0] = part("fetched", r, t0)
-            nc.scalar.activation(fetched[r, t0][:], listed(r, t0), COPY)
-
-        def fetch_gated(r, t0):
-            gated[r, t0] = part("gated", r, t0)
-            nc.vector.tensor_tensor(gated[r, t0][:], listed(r, t0), gate_sb[r][:, t0 : t0 + HALF], MULT)
+            places = pos_sb[r][:, t0 // 16 : (t0 + HALF) // 16]
+            nc.scalar.activation(fetched[r, t0][:], y_all[:].indirect(places), COPY)
 
         def apply_gate(r, t0):
             gated[r, t0] = part("gated", r, t0)
             nc.vector.tensor_tensor(gated[r, t0][:], fetched[r, t0][:], gate_sb[r][:, t0 : t0 + HALF], MULT)
 
-        def add(name, t0, first, second):
-            total = part(name, 0, t0)
-            nc.vector.tensor_tensor(total[:], first[:], second[:], ADD)
-            return total
+        def add(r, t0, so_far):
+            total = part("total", r, t0)
+            nc.vector.tensor_tensor(total[:], so_far, gated[r, t0][:], ADD)
+            return total[:]
 
         for r, t0 in ((1, 0), (2, 0), (1, HALF), (2, HALF)):
             fetch(r, t0)
-        fetch_gated(0, 0)
-        fetch_gated(0, HALF)
+        nc.vector.tensor_tensor(first[:], y_all[:].indirect(pos_sb[0][:]), gate_sb[0][:], MULT)
         apply_gate(1, 0)
         apply_gate(2, 0)
-        two = add("two", 0, gated[0, 0], gated[1, 0])
+        two = add(1, 0, first[:, :HALF])
         apply_gate(1, HALF)
-        nc.sync.dma_start(out[:, :HALF], add("three", 0, two, gated[2, 0])[:])
-        two = add("two", HALF, gated[0, HALF], gated[1, HALF])
-        apply_gate(2, HALF)
-        nc.sync.dma_start(out[:, HALF:], add("three", HALF, two, gated[2, HALF])[:])
+        nc.sync.dma_start(out[:, :HALF], add(2, 0, two))
+        two = add(1, HALF, first[:, HALF:])
+        last, total = part("gated", 2, HALF), part("total", 2, HALF)
+        quarters = (slice(0, HALF // 2), slice(HALF // 2, HALF))
+        for cols in quarters:
+            nc.vector.tensor_tensor(last[:, cols], fetched[2, HALF][:, cols], gate_sb[2][:, HALF:][:, cols], MULT)
+        for cols in quarters:
+            nc.vector.tensor_tensor(total[:, cols], two[:, cols], last[:, cols], ADD)
+        nc.sync.dma_start(out[:, HALF:], total[:])

@@ -30,8 +30,10 @@ X_VECTOR = 160
 GATHERED = [(0,), (1, 2), (3, 4, 5), (6, 7, 8), (9, 10, 11)]
 S1_CUTS = (0, 6, E)
 ON_GPSIMD = 2
+S3_CUT = 2
 HALF = 256
 TURNED = [(0, 1), (2, 3), (4, 5), (6, 7), (8, 9), (10,), (11,)]
+QUANTISED = [(0, 1, 2, 3), (4, 5, 6, 7), (8, 9), (10,), (11,)]
 
 
 def tile_moe_tk_glu_relu_kernel(
@@ -51,7 +53,7 @@ def tile_moe_tk_glu_relu_kernel(
             return tile
 
         s1 = [scale_tile("s1", s1_of, H, e0, e1) for e0, e1 in zip(S1_CUTS, S1_CUTS[1:])]
-        s3_early, s3_late = scale_tile("s3", s3_of, H, 0, ON_GPSIMD), scale_tile("s3", s3_of, H, ON_GPSIMD, E)
+        s3_early, s3_late = scale_tile("s3", s3_of, H, 0, S3_CUT), scale_tile("s3", s3_of, H, S3_CUT, E)
         s2 = scale_tile("s2", s2_of, N, 0, E)
         x_words = held.tile([P, T], U32, name="x_words", align_bytes=64)
         x_scales = held.tile([P, T], U8, name="x_scales", align_bytes=64)
@@ -67,7 +69,7 @@ def tile_moe_tk_glu_relu_kernel(
 
         make_identity(nc, ident[:])
         nc.vector.memset(as_int32(s3_late), 0)
-        load_scales(nc.gpsimd, s3_late, w3_scales, ON_GPSIMD, E)
+        load_scales(nc.gpsimd, s3_late, w3_scales, S3_CUT, E)
         nc.gpsimd.memset(as_int32(s2), 0)
         for zeroed in (as_int32(s1[0]), as_int32(s3_early), x_scales[:].bitcast(I32), as_int32(s1[1])):
             cut = zeroed.shape[1] // 2 - 1
@@ -86,7 +88,7 @@ def tile_moe_tk_glu_relu_kernel(
 
         def load_words(name, words, by_expert, width, experts):
             e0, n = experts[0], len(experts)
-            w = held.tile([P, n, 2 * width], U8, name=f"{name}_{e0}", align_bytes=64)
+            w = held.tile([P, n, 2 * width], U8, name=f"{name}_{e0}", tag=f"{name}_{e0}", align_bytes=64)
             nc.sync.dma_start(w[:].bitcast(I32), words[e0 : e0 + n, 0].rearrange("e p b -> p e b").bitcast(I32))
             for k in range(n):
                 by_expert[e0 + k] = w[:, k, :]
@@ -105,23 +107,23 @@ def tile_moe_tk_glu_relu_kernel(
 
         load_s1(0)
         load_w1(0)
-        load_scales(nc.sync, s3_early, w3_scales, 0, ON_GPSIMD)
+        load_scales(nc.sync, s3_early, w3_scales, 0, S3_CUT)
         load_w3(0, 1)
         load_w1(1, 2)
         load_w1(3, 4, 5)
+        load_w3(2, 3, 4)
         load_s1(1)
-        load_w1(6, 7, 8)
-        load_w3(2, 3)
+        load_w1(6, 7)
+        load_w3(5, 6)
+        load_w1(8, 9)
+        load_w3(7, 8)
+        load_w1(10, 11)
+        load_w3(9, 10, 11)
         pos_sb = []
         for r, pos in enumerate((pos1, pos2, pos3)):
             places = held.tile([P, T // 16], U16, name=f"pos_sb_{r}")
             nc.sync.dma_start(places[:], pos)
             pos_sb.append(places)
-        load_w1(9, 10, 11)
-        load_w3(4, 5)
-        load_w3(6, 7)
-        load_w3(8, 9)
-        load_w3(10, 11)
         load_scales(nc.sync, s2, w2_scales, 0, E)
         load_w2(0, 1, 2, 3, 4, 5)
         load_w2(6, 7, 8, 9, 10, 11)
@@ -144,14 +146,20 @@ def tile_moe_tk_glu_relu_kernel(
             )
 
         relu_of, b_of, h_of, rows_of, h_mx = {}, {}, {}, {}, {}
+        for group in QUANTISED:
+            rows = held.tile([P, len(group), C, PACK], BF16, name=f"h_rows_{group[0]}", align_bytes=64)
+            for k, e in enumerate(group):
+                rows_of[e] = (rows, k)
         y_all = held.tile([N, S], F32, name="y_all")
 
         x_mx = {}
-        for group in GATHERED:
+
+        def gather(g, codes_on=None, scales_on=None):
+            group = GATHERED[g]
             e0, n = group[0], len(group)
             slots = offs_sb[:, e0 * C // 16 : (e0 + n) * C // 16]
-            codes = held.tile([P, n * C], U32, name=f"codes_{e0}", align_bytes=64)
-            scales = held.tile([P, n * C], U8, name=f"scales_{e0}", align_bytes=64)
+            codes = held.tile([P, n * C], U32, name=f"codes_{e0}", tag=codes_on or f"codes_{e0}", align_bytes=64)
+            scales = held.tile([P, n * C], U8, name=f"scales_{e0}", tag=scales_on or f"scales_{e0}", align_bytes=64)
             nc.vector.tensor_copy(codes[:], x_words[:].indirect(slots))
             nc.vector.tensor_copy(scales[:], x_scales[:].indirect(slots))
             for k, e in enumerate(group):
@@ -202,18 +210,18 @@ def tile_moe_tk_glu_relu_kernel(
                 words = h_of[e][:].rearrange("c u p v -> c (u p v)").bitcast(F32)
                 for u in range(2):
                     nc.tensor.transpose(turned[:, k, u, :], words[:, u * P : (u + 1) * P], ident[:])
-            rows_of[g] = held.tile([P, len(group), C, PACK], BF16, name=f"h_rows_{g}", align_bytes=64)
-            nc.scalar.copy(rows_of[g][:].bitcast(F32), turned[:].rearrange("p k u c -> p k c u"))
+            tile, k0 = rows_of[group[0]]
+            nc.scalar.copy(tile[:, k0 : k0 + len(group)].bitcast(F32), turned[:].rearrange("p k u c -> p k c u"))
 
         def quantise_h(g, after=None):
-            group = TURNED[g]
+            group = QUANTISED[g]
             tag = f"h_codes_{g}" if after is None else f"relu_a_{after}"
             h_codes = held.tile([P, len(group) * C], U32, name=f"h_codes_{g}", tag=tag, align_bytes=64)
             h_scales = held.tile([P, len(group) * C], U8, name=f"h_scales_{g}", align_bytes=64)
             nc.vector.quantize_mx(
                 out=h_codes[:].bitcast(FP8X4),
                 scales=h_scales[:],
-                in_=rows_of[g][:].rearrange("p k c j -> p (k c j)"),
+                in_=rows_of[group[0]][0][:].rearrange("p k c j -> p (k c j)"),
             )
             for k, e in enumerate(group):
                 h_mx[e] = (h_codes[:, k * C : (k + 1) * C], h_scales[:, k * C : (k + 1) * C])
@@ -232,41 +240,44 @@ def tile_moe_tk_glu_relu_kernel(
                 )
             empty(y_all[:, experts[0] * C : (experts[-1] + 1) * C], y[:])
 
-        for e, bank in zip(range(ON_GPSIMD), (7, 3)):
-            relu_a((e,), banks=(e,))
-            product_on_gpsimd(e, bank)
-        relu_a(range(2, 9), banks=(2, 0, 1, 2, 0, 1, 7))
-        make_b((2, 3), banks=(3, 4))
-        relu_a((9, 10, 11), banks=(2, 0, 1))
-        make_b((4, 5, 6), banks=(5, 6, 7))
-        product(2)
-        make_b((7,), banks=(3,))
-        product(3)
-        turn(0, bank=2)
-        turn(1, bank=0)
-        make_b((8,), banks=(4,))
-        product(4, 5)
-        turn(2, bank=1)
-        make_b((9, 10), banks=(5, 6))
-        product(6, 7)
-        turn(3, bank=2)
-        make_b((11,), banks=(7,))
-        quantise_h(0)
-        quantise_h(1)
-        second_layer((0, 1, 2, 3), 3, nc.scalar.copy)
-        product(8, 9)
-        turn(4, bank=0)
-        product(10)
-        turn(5, bank=1)
-        product(11)
-        turn(6, bank=4)
-        quantise_h(2, after=9)
-        quantise_h(3, after=10)
-        for g in range(4, len(TURNED)):
+        for g in range(4):
+            gather(g)
+        relu_a((0,), banks=(0,))
+        product_on_gpsimd(0, 3)
+        relu_a((1,), banks=(1,))
+        product_on_gpsimd(1, 4)
+        relu_a((2, 3, 4), banks=(2, 0, 1))
+        make_b((2, 3, 4), banks=(5, 6, 7))
+        relu_a((5,), banks=(2,))
+        product(2, 3, 4)
+        relu_a((6, 7), banks=(0, 1))
+        make_b((5,), banks=(2,))
+        product(5)
+        product_on_gpsimd(6, 3)
+        gather(4, codes_on="w3_5", scales_on="w1_6")
+        turn(0, bank=0)
+        turn(1, bank=1)
+        relu_a((8,), banks=(4,))
+        make_b((7, 8), banks=(5, 6))
+        product(7, 8)
+        turn(2, bank=7)
+        relu_a((9, 10), banks=(2, 3))
+        make_b((9,), banks=(0,))
+        relu_a((11,), banks=(4,))
+        make_b((10, 11), banks=(1, 5))
+        quantise_h(0, after=8)
+        product(9)
+        turn(3, bank=6)
+        turn(4, bank=7)
+        product(10, 11)
+        turn(5, bank=2)
+        turn(6, bank=3)
+        for g in range(1, len(QUANTISED)):
             quantise_h(g)
-        second_layer((4, 5, 6, 7), 2, nc.vector.tensor_copy)
-        second_layer((8, 9, 10), 5, nc.scalar.copy)
-        second_layer((11,), 6, nc.vector.tensor_copy)
+        second_layer((0, 1, 2, 3), 0, nc.scalar.copy)
+        second_layer((4, 5, 6, 7), 4, nc.vector.tensor_copy)
+        second_layer((8, 9, 10), 1, nc.scalar.copy)
+        second_layer((11,), 5, nc.vector.tensor_copy)
 
         first = held.tile([N, T], F32, name="first")
         fetched, gated = {}, {}

@@ -26,7 +26,7 @@ COPY = mybir.ActivationFunctionType.Copy
 
 BANK = 2048
 X_TOKENS = 256
-X_VECTOR = 160
+X_SCALAR = 192
 GATHERED = [(0,), (1, 2), (3, 4, 5), (6, 7, 8), (9, 10, 11)]
 S1_CUTS = (0, 6, E)
 ON_GPSIMD = 2
@@ -70,17 +70,14 @@ def tile_moe_tk_glu_relu_kernel(
         make_identity(nc, ident[:])
         nc.vector.memset(as_int32(s3_late), 0)
         load_scales(nc.gpsimd, s3_late, w3_scales, S3_CUT, E)
-        nc.gpsimd.memset(as_int32(s2), 0)
-        for zeroed in (as_int32(s1[0]), as_int32(s3_early), x_scales[:].bitcast(I32), as_int32(s1[1])):
+        for zeroed in (as_int32(s1[0]), as_int32(s3_early), x_scales[:].bitcast(I32), as_int32(s1[1]), as_int32(s2)):
             cut = zeroed.shape[1] // 2 - 1
             nc.vector.memset(zeroed[:, :cut], 0)
             nc.vector.memset(zeroed[:, cut:], 0)
 
         x_rows = xT.rearrange("(p j) t -> p j t", j=PACK)
-        x_f32 = {}
-        for t0 in range(0, T, X_TOKENS):
-            x_f32[t0] = held.tile([P, PACK, X_TOKENS], F32, name=f"x_f32_{t0}", align_bytes=64)
-            nc.sync.dma_start(x_f32[t0][:], x_rows[:, :, t0 : t0 + X_TOKENS])
+        x_f32 = held.tile([P, PACK, T], F32, name="x_f32", align_bytes=64)
+        nc.sync.dma_start(x_f32[:], x_rows)
         offs_sb = held.tile([P, S // 16], U16, name="offs_sb")
         nc.sync.dma_start(offs_sb[:], offs)
 
@@ -132,12 +129,11 @@ def tile_moe_tk_glu_relu_kernel(
             gate_sb.append(held.tile([N, T], F32, name=f"gate_sb_{r}"))
             nc.sync.dma_start(gate_sb[r][:], gate[r])
 
-        x_bf16 = {}
-        for t0, chunk in x_f32.items():
-            x_bf16[t0] = held.tile([P, X_TOKENS, PACK], BF16, name=f"x_bf16_{t0}", align_bytes=64)
-            by_token = chunk[:].rearrange("p j t -> p t j")
-            nc.vector.tensor_copy(x_bf16[t0][:, :X_VECTOR, :], by_token[:, :X_VECTOR, :])
-            nc.scalar.copy(x_bf16[t0][:, X_VECTOR:, :], by_token[:, X_VECTOR:, :])
+        x_bf16 = {t0: held.tile([P, X_TOKENS, PACK], BF16, name=f"x_bf16_{t0}", align_bytes=64) for t0 in (0, X_TOKENS)}
+        by_token = x_f32[:].rearrange("p j t -> p t j")
+        nc.vector.tensor_copy(x_bf16[0][:], by_token[:, :X_TOKENS, :])
+        nc.scalar.copy(x_bf16[X_TOKENS][:, :X_SCALAR, :], by_token[:, X_TOKENS : X_TOKENS + X_SCALAR, :])
+        nc.vector.tensor_copy(x_bf16[X_TOKENS][:, X_SCALAR:, :], by_token[:, X_TOKENS + X_SCALAR :, :])
         for t0, rounded in x_bf16.items():
             nc.vector.quantize_mx(
                 out=x_words[:, t0 : t0 + X_TOKENS].bitcast(FP8X4),
@@ -242,42 +238,41 @@ def tile_moe_tk_glu_relu_kernel(
 
         for g in range(4):
             gather(g)
+        gather(4)
         relu_a((0,), banks=(0,))
         product_on_gpsimd(0, 3)
         relu_a((1,), banks=(1,))
         product_on_gpsimd(1, 4)
-        relu_a((2, 3, 4), banks=(2, 0, 1))
-        make_b((2, 3, 4), banks=(5, 6, 7))
-        relu_a((5,), banks=(2,))
-        product(2, 3, 4)
+        relu_a((2, 3, 4, 5), banks=(2, 0, 1, 5))
+        product_on_gpsimd(4, 3)
+        make_b((2, 3), banks=(6, 7))
+        product(2, 3)
         relu_a((6, 7), banks=(0, 1))
-        make_b((5,), banks=(2,))
-        product(5)
-        product_on_gpsimd(6, 3)
-        gather(4, codes_on="w3_5", scales_on="w1_6")
+        make_b((5, 6), banks=(2, 4))
+        product(5, 6)
         turn(0, bank=0)
         turn(1, bank=1)
-        relu_a((8,), banks=(4,))
-        make_b((7, 8), banks=(5, 6))
+        relu_a((8,), banks=(5,))
+        make_b((7, 8), banks=(3, 6))
         product(7, 8)
         turn(2, bank=7)
-        relu_a((9, 10), banks=(2, 3))
+        relu_a((9, 10), banks=(2, 4))
         make_b((9,), banks=(0,))
-        relu_a((11,), banks=(4,))
-        make_b((10, 11), banks=(1, 5))
+        relu_a((11,), banks=(5,))
+        make_b((10, 11), banks=(1, 3))
         quantise_h(0, after=8)
         product(9)
         turn(3, bank=6)
         turn(4, bank=7)
         product(10, 11)
         turn(5, bank=2)
-        turn(6, bank=3)
+        turn(6, bank=4)
         for g in range(1, len(QUANTISED)):
             quantise_h(g)
         second_layer((0, 1, 2, 3), 0, nc.scalar.copy)
-        second_layer((4, 5, 6, 7), 4, nc.vector.tensor_copy)
+        second_layer((4, 5, 6, 7), 5, nc.vector.tensor_copy)
         second_layer((8, 9, 10), 1, nc.scalar.copy)
-        second_layer((11,), 5, nc.vector.tensor_copy)
+        second_layer((11,), 3, nc.vector.tensor_copy)
 
         first = held.tile([N, T], F32, name="first")
         fetched, gated = {}, {}

from contextlib import ExitStack

import concourse.mybir as mybir
from concourse.masks import make_identity

K, T, E, C, H, N = 512, 512, 12, 128, 512, 128
TOP = 3
S = E * C
P = 128
PACK = 4

FLOPS = 2 * S * (2 * K * H + H * N)

F32 = mybir.dt.float32
BF16 = mybir.dt.bfloat16
I32 = mybir.dt.int32
U32 = mybir.dt.uint32
U16 = mybir.dt.uint16
U8 = mybir.dt.uint8
FP8X4 = mybir.dt.float8_e4m3fn_x4
FP4X4 = mybir.dt.float4_e2m1fn_x4
MULT = mybir.AluOpType.mult
ADD = mybir.AluOpType.add
RELU = mybir.ActivationFunctionType.Relu
COPY = mybir.ActivationFunctionType.Copy

BANK = 2048
X_TOKENS = 256
X_SCALAR = 192
GATHERED = [(0,), (1, 2), (3, 4, 5), (6, 7, 8), (9, 10, 11)]
S1_CUTS = (0, 6, E)
ON_GPSIMD = 2
S3_CUT = 2
HALF = 256
TURNED = [(0, 1), (2, 3), (4, 5), (6, 7), (8, 9), (10,), (11,)]
QUANTISED = [(0, 1, 2, 3), (4, 5, 6, 7), (8, 9), (10,), (11,)]


def tile_moe_tk_glu_relu_kernel(
    tc, xT, w1_words, w1_scales, w3_words, w3_scales, w2_words, w2_scales, gate, offs, pos1, pos2, pos3, out
):
    nc = tc.nc
    with ExitStack() as ctx:
        held = ctx.enter_context(tc.tile_pool(name="held", bufs=1))
        psum = ctx.enter_context(tc.psum_pool(name="psum", bufs=1))

        s1_of, s3_of, s2_of = {}, {}, {}

        def scale_tile(name, by_expert, width, e0, e1):
            tile = held.tile([P, e1 - e0, width], U8, name=f"{name}_{e0}", align_bytes=64)
            for e in range(e0, e1):
                by_expert[e] = tile[:, e - e0, :]
            return tile

        s1 = [scale_tile("s1", s1_of, H, e0, e1) for e0, e1 in zip(S1_CUTS, S1_CUTS[1:])]
        s3_early, s3_late = scale_tile("s3", s3_of, H, 0, S3_CUT), scale_tile("s3", s3_of, H, S3_CUT, E)
        s2 = scale_tile("s2", s2_of, N, 0, E)
        x_words = held.tile([P, T], U32, name="x_words", align_bytes=64)
        x_scales = held.tile([P, T], U8, name="x_scales", align_bytes=64)
        ident = held.tile([P, P], F32, name="ident")

        def as_int32(scales):
            return scales[:].rearrange("p e i -> p (e i)").bitcast(I32)

        def load_scales(queue, tile, scales, e0, e1):
            rows = scales[e0:e1, 0].rearrange("e (q r) i -> r q e i", r=4)
            for r in range(4):
                queue.dma_start(tile[r:P:32, :, :].bitcast(I32), rows[r].bitcast(I32))

        make_identity(nc, ident[:])
        nc.vector.memset(as_int32(s3_late), 0)
        load_scales(nc.gpsimd, s3_late, w3_scales, S3_CUT, E)
        for zeroed in (as_int32(s1[0]), as_int32(s3_early), x_scales[:].bitcast(I32), as_int32(s1[1]), as_int32(s2)):
            cut = zeroed.shape[1] // 2 - 1
            nc.vector.memset(zeroed[:, :cut], 0)
            nc.vector.memset(zeroed[:, cut:], 0)

        x_rows = xT.rearrange("(p j) t -> p j t", j=PACK)
        x_f32 = held.tile([P, PACK, T], F32, name="x_f32", align_bytes=64)
        nc.sync.dma_start(x_f32[:], x_rows)
        offs_sb = held.tile([P, S // 16], U16, name="offs_sb")
        nc.sync.dma_start(offs_sb[:], offs)

        w1_sb, w3_sb, w2_sb = {}, {}, {}

        def load_words(name, words, by_expert, width, experts):
            e0, n = experts[0], len(experts)
            w = held.tile([P, n, 2 * width], U8, name=f"{name}_{e0}", tag=f"{name}_{e0}", align_bytes=64)
            nc.sync.dma_start(w[:].bitcast(I32), words[e0 : e0 + n, 0].rearrange("e p b -> p e b").bitcast(I32))
            for k in range(n):
                by_expert[e0 + k] = w[:, k, :]

        def load_w1(*experts):
            load_words("w1", w1_words, w1_sb, H, experts)

        def load_w3(*experts):
            load_words("w3", w3_words, w3_sb, H, experts)

        def load_w2(*experts):
            load_words("w2", w2_words, w2_sb, N, experts)

        def load_s1(k):
            load_scales(nc.sync, s1[k], w1_scales, S1_CUTS[k], S1_CUTS[k + 1])

        load_s1(0)
        load_w1(0)
        load_scales(nc.sync, s3_early, w3_scales, 0, S3_CUT)
        load_w3(0, 1)
        load_w1(1, 2)
        load_w1(3, 4, 5)
        load_w3(2, 3, 4)
        load_s1(1)
        load_w1(6, 7)
        load_w3(5, 6)
        load_w1(8, 9)
        load_w3(7, 8)
        load_w1(10, 11)
        load_w3(9, 10, 11)
        pos_sb = []
        for r, pos in enumerate((pos1, pos2, pos3)):
            places = held.tile([P, T // 16], U16, name=f"pos_sb_{r}")
            nc.sync.dma_start(places[:], pos)
            pos_sb.append(places)
        load_scales(nc.sync, s2, w2_scales, 0, E)
        load_w2(0, 1, 2, 3, 4, 5)
        load_w2(6, 7, 8, 9, 10, 11)
        gate_sb = []
        for r in range(TOP):
            gate_sb.append(held.tile([N, T], F32, name=f"gate_sb_{r}"))
            nc.sync.dma_start(gate_sb[r][:], gate[r])

        x_bf16 = {t0: held.tile([P, X_TOKENS, PACK], BF16, name=f"x_bf16_{t0}", align_bytes=64) for t0 in (0, X_TOKENS)}
        by_token = x_f32[:].rearrange("p j t -> p t j")
        nc.vector.tensor_copy(x_bf16[0][:], by_token[:, :X_TOKENS, :])
        nc.scalar.copy(x_bf16[X_TOKENS][:, :X_SCALAR, :], by_token[:, X_TOKENS : X_TOKENS + X_SCALAR, :])
        nc.vector.tensor_copy(x_bf16[X_TOKENS][:, X_SCALAR:, :], by_token[:, X_TOKENS + X_SCALAR :, :])
        for t0, rounded in x_bf16.items():
            nc.vector.quantize_mx(
                out=x_words[:, t0 : t0 + X_TOKENS].bitcast(FP8X4),
                scales=x_scales[:, t0 : t0 + X_TOKENS],
                in_=rounded[:].rearrange("p t j -> p (t j)"),
            )

        relu_of, b_of, h_of, rows_of, h_mx = {}, {}, {}, {}, {}
        for group in QUANTISED:
            rows = held.tile([P, len(group), C, PACK], BF16, name=f"h_rows_{group[0]}", align_bytes=64)
            for k, e in enumerate(group):
                rows_of[e] = (rows, k)
        y_all = held.tile([N, S], F32, name="y_all")

        x_mx = {}

        def gather(g, codes_on=None, scales_on=None):
            group = GATHERED[g]
            e0, n = group[0], len(group)
            slots = offs_sb[:, e0 * C // 16 : (e0 + n) * C // 16]
            codes = held.tile([P, n * C], U32, name=f"codes_{e0}", tag=codes_on or f"codes_{e0}", align_bytes=64)
            scales = held.tile([P, n * C], U8, name=f"scales_{e0}", tag=scales_on or f"scales_{e0}", align_bytes=64)
            nc.vector.tensor_copy(codes[:], x_words[:].indirect(slots))
            nc.vector.tensor_copy(scales[:], x_scales[:].indirect(slots))
            for k, e in enumerate(group):
                x_mx[e] = (codes[:, k * C : (k + 1) * C], scales[:, k * C : (k + 1) * C])

        def by_pairs(acc):
            return acc.rearrange("c (p u v) -> c u p v", u=2, v=2)

        def first_layer(name, e, bank, words, scales):
            acc = psum.tile([C, H], F32, name=f"{name}_{e}", offset=bank * BANK)
            nc.tensor.matmul_mx(
                out=acc[:],
                lhsT=x_mx[e][0].bitcast(FP8X4),
                lhsT_scale=x_mx[e][1],
                rhs=words.bitcast(FP4X4),
                rhs_scale=scales,
                start=True,
                stop=True,
            )
            return acc

        def relu_a(experts, banks):
            for e, bank in zip(experts, banks):
                a = first_layer("a", e, bank, w1_sb[e], s1_of[e])
                relu_of[e] = held.tile([C, 2, P, 2], F32, name=f"relu_a_{e}", tag=f"relu_a_{e}", align_bytes=64)
                nc.scalar.activation(relu_of[e][:], by_pairs(a[:]), RELU)

        def make_b(experts, banks):
            for e, bank in zip(experts, banks):
                b_of[e] = first_layer("b", e, bank, w3_sb[e], s3_of[e])

        def product(*experts):
            for e in experts:
                h_of[e] = held.tile([C, 2, P, 2], BF16, name=f"h_{e}")
                nc.vector.tensor_tensor(h_of[e][:], by_pairs(b_of[e][:]), relu_of[e][:], MULT)

        def product_on_gpsimd(e, bank):
            make_b((e,), (bank,))
            b_sb = held.tile([C, 2, P, 2], F32, name=f"b_sb_{e}")
            nc.scalar.copy(b_sb[:], by_pairs(b_of[e][:]))
            h_of[e] = held.tile([C, 2, P, 2], BF16, name=f"h_{e}")
            nc.gpsimd.tensor_tensor(h_of[e][:], b_sb[:], relu_of[e][:], MULT)

        def turn(g, bank):
            group = TURNED[g]
            turned = psum.tile([P, len(group), 2, C], F32, name=f"turned_{g}", offset=bank * BANK)
            for k, e in reversed(list(enumerate(group))):
                words = h_of[e][:].rearrange("c u p v -> c (u p v)").bitcast(F32)
                for u in range(2):
                    nc.tensor.transpose(turned[:, k, u, :], words[:, u * P : (u + 1) * P], ident[:])
            tile, k0 = rows_of[group[0]]
            nc.scalar.copy(tile[:, k0 : k0 + len(group)].bitcast(F32), turned[:].rearrange("p k u c -> p k c u"))

        def quantise_h(g, after=None):
            group = QUANTISED[g]
            tag = f"h_codes_{g}" if after is None else f"relu_a_{after}"
            h_codes = held.tile([P, len(group) * C], U32, name=f"h_codes_{g}", tag=tag, align_bytes=64)
            h_scales = held.tile([P, len(group) * C], U8, name=f"h_scales_{g}", align_bytes=64)
            nc.vector.quantize_mx(
                out=h_codes[:].bitcast(FP8X4),
                scales=h_scales[:],
                in_=rows_of[group[0]][0][:].rearrange("p k c j -> p (k c j)"),
            )
            for k, e in enumerate(group):
                h_mx[e] = (h_codes[:, k * C : (k + 1) * C], h_scales[:, k * C : (k + 1) * C])

        def second_layer(experts, bank, empty):
            y = psum.tile([N, len(experts) * C], F32, name=f"y_{experts[0]}", offset=bank * BANK)
            for k, e in enumerate(experts):
                nc.tensor.matmul_mx(
                    out=y[:, k * C : (k + 1) * C],
                    lhsT=w2_sb[e].bitcast(FP4X4),
                    lhsT_scale=s2_of[e],
                    rhs=h_mx[e][0].bitcast(FP8X4),
                    rhs_scale=h_mx[e][1],
                    start=True,
                    stop=True,
                )
            empty(y_all[:, experts[0] * C : (experts[-1] + 1) * C], y[:])

        for g in range(4):
            gather(g)
        gather(4)
        relu_a((0,), banks=(0,))
        product_on_gpsimd(0, 3)
        relu_a((1,), banks=(1,))
        product_on_gpsimd(1, 4)
        relu_a((2, 3, 4, 5), banks=(2, 0, 1, 5))
        product_on_gpsimd(4, 3)
        make_b((2, 3), banks=(6, 7))
        product(2, 3)
        relu_a((6, 7), banks=(0, 1))
        make_b((5, 6), banks=(2, 4))
        product(5, 6)
        turn(0, bank=0)
        turn(1, bank=1)
        relu_a((8,), banks=(5,))
        make_b((7, 8), banks=(3, 6))
        product(7, 8)
        turn(2, bank=7)
        relu_a((9, 10), banks=(2, 4))
        make_b((9,), banks=(0,))
        relu_a((11,), banks=(5,))
        make_b((10, 11), banks=(1, 3))
        quantise_h(0, after=8)
        product(9)
        turn(3, bank=6)
        turn(4, bank=7)
        product(10, 11)
        turn(5, bank=2)
        turn(6, bank=4)
        for g in range(1, len(QUANTISED)):
            quantise_h(g)
        second_layer((0, 1, 2, 3), 0, nc.scalar.copy)
        second_layer((4, 5, 6, 7), 5, nc.vector.tensor_copy)
        second_layer((8, 9, 10), 1, nc.scalar.copy)
        second_layer((11,), 3, nc.vector.tensor_copy)

        first = held.tile([N, T], F32, name="first")
        fetched, gated = {}, {}

        def part(name, r, t0):
            return held.tile([N, HALF], F32, name=f"{name}_{r}_{t0}")

        def fetch(r, t0):
            fetched[r, t0] = part("fetched", r, t0)
            places = pos_sb[r][:, t0 // 16 : (t0 + HALF) // 16]
            nc.scalar.activation(fetched[r, t0][:], y_all[:].indirect(places), COPY)

        def apply_gate(r, t0):
            gated[r, t0] = part("gated", r, t0)
            nc.vector.tensor_tensor(gated[r, t0][:], fetched[r, t0][:], gate_sb[r][:, t0 : t0 + HALF], MULT)

        def add(r, t0, so_far):
            total = part("total", r, t0)
            nc.vector.tensor_tensor(total[:], so_far, gated[r, t0][:], ADD)
            return total[:]

        for r, t0 in ((1, 0), (2, 0), (1, HALF), (2, HALF)):
            fetch(r, t0)
        nc.vector.tensor_tensor(first[:], y_all[:].indirect(pos_sb[0][:]), gate_sb[0][:], MULT)
        apply_gate(1, 0)
        apply_gate(2, 0)
        two = add(1, 0, first[:, :HALF])
        apply_gate(1, HALF)
        nc.sync.dma_start(out[:, :HALF], add(2, 0, two))
        two = add(1, HALF, first[:, HALF:])
        last, total = part("gated", 2, HALF), part("total", 2, HALF)
        quarters = (slice(0, HALF // 2), slice(HALF // 2, HALF))
        for cols in quarters:
            nc.vector.tensor_tensor(last[:, cols], fetched[2, HALF][:, cols], gate_sb[2][:, HALF:][:, cols], MULT)
        for cols in quarters:
            nc.vector.tensor_tensor(total[:, cols], two[:, cols], last[:, cols], ADD)
        nc.sync.dma_start(out[:, HALF:], total[:])
